import numpy as np, ml_dtypes
CORES = [1,5,17,21,33,37,49,53]
N = 8
import mx_ref
BF = ml_dtypes.bfloat16
def pick(q, e):
    c = np.concatenate([q[0].reshape(128, -1, 4), np.zeros((128, 1, 4), np.uint8)], axis=1); s = np.concatenate([q[1], np.ones((16, 1), np.uint8)], axis=1)
    return (np.ascontiguousarray(c[:, e].reshape(128, -1)), np.ascontiguousarray(s[:, e]))
def join(*qs):
    return (np.concatenate([q[0] for q in qs], axis=1), np.concatenate([q[1] for q in qs], axis=1))
def put(q, e, v):
    c, s = q[0].reshape(128, -1, 4).copy(), q[1].copy(); c[:, e] = v[0].reshape(128, -1, 4); s[:, e] = v[1]
    return (c.reshape(128, -1), s)
def pk(c, s):
    return (np.ascontiguousarray(c), mx_ref.live(s))
def emit(q):
    return q[0], q[1]
def cut(t, i, w=512):
    return t[:, w * i:w * i + w]
def f(rng, *shape):
    return mx_ref.flush((rng.standard_normal(shape, dtype=np.float32) * np.exp2(rng.integers(-2, 3, shape[:-1] + (1,)))).astype(BF))
def wide(rng, *shape, cols=0):
    v = rng.standard_normal(shape, dtype=np.float32) * np.exp2(rng.integers(-12, 13, shape)).astype(np.float32)
    if cols: v *= np.repeat(np.exp2(rng.integers(-cols, cols + 1, shape[:-2] + (1, shape[-1] // 4))) * (rng.random(shape[:-2] + (1, shape[-1] // 4)) > 0.0625), 4, axis=-1).astype(np.float32)
    return mx_ref.flush(v.astype(BF))
P, R, O = 1024, 4, 2
C = P // 16
CLOUD = np.arange(N * P) % P // C
def same(t):
    return np.stack([t] * N)
def sizes(rng, *shape):
    return (1 + rng.random(shape, dtype=np.float32)) * (1 - 2 * rng.integers(0, 2, shape)).astype(np.float32)
def setup_inputs(rng):
    return {"x": f(rng, N, 128, 4 * P), "seed": same(f(rng, 128, 64)), "w": f(rng, N, 128, 512 * O)}
def setup_inputs_again(rng):
    d = setup_inputs(rng)
    half = rng.permutation(16) < 8
    four = rng.permutation(np.flatnonzero(half))[:4]
    huge, minus = np.isin(np.arange(16), four), np.isin(np.arange(16), four[:2])
    x, s = sizes(rng, N, 128, 4 * P), sizes(rng, 128, 64)
    x = np.where(np.repeat(half, 4 * C), np.abs(x), x)
    s = np.where(np.repeat(half, 4), np.abs(s), s)
    for b in np.flatnonzero(half):
        r, j = int(rng.integers(0, N)), int(b * C + rng.integers(0, C))
        if minus[b]: r, j = 0, int(b * C)
        x[r, :, 4 * j:4 * j + 4] *= np.float32(0.5 if huge[b] else 2.0 ** -8)
    by = np.where(huge, np.float32(2.0 ** 29), np.float32(1))
    x, s = x * np.repeat(by, 4 * C), s * np.repeat(np.where(minus, -by, by), 4)
    d["x"], d["seed"] = x.astype(BF), same(s.astype(BF))
    return d
def setup_inputs_late(rng):
    d = setup_inputs(rng)
    top = (np.arange(128) < 64)[:, None]
    a = np.stack([rng.permutation(C) < C // 2 for i in range(16 * N)]).reshape(N, 1, P)
    a = np.repeat(a, 4, axis=2)
    v = sizes(rng, N, 128, 4 * P)
    d["x"] = np.where(top, np.where(a, -np.abs(v), v * np.float32(2.0 ** -6)), np.where(a, 0, v)).astype(BF)
    d["seed"] = same(np.where(top, np.abs(sizes(rng, 128, 64)), 0).astype(BF))
    return d
def setup_inputs_one(rng):
    d = setup_inputs(rng)
    h = int(rng.integers(0, N))
    s = sizes(rng, 128, 64).astype(BF)
    d["seed"] = same(s)
    d["x"] = same(np.repeat(s.reshape(128, 16, 1, 4), C, axis=2).reshape(128, 4 * P))
    d["x"][h] = (sizes(rng, 128, 4 * P) * np.float32(2.0 ** -6)).astype(BF)
    return d
def setup_inputs_spread(rng):
    d = setup_inputs(rng)
    x, s = wide(rng, N, 128, 4 * P, cols=6).astype(np.float32), wide(rng, 128, 64).astype(np.float32)
    plus = rng.permutation(16) < 4
    x = np.where(np.repeat(plus, 4 * C), np.abs(x), x)
    s = np.where(np.repeat(plus, 4), np.abs(s), s)
    for b in np.flatnonzero(plus):
        for r, zero in zip(np.sort(rng.permutation(N)[:2]), (0.0, -0.0)):
            j = int(b * C + rng.integers(0, C))
            x[r, :, 4 * j:4 * j + 4] = np.float32(zero)
    d["x"], d["seed"] = x.astype(BF), same(s.astype(BF))
    return d
def setup_inputs_ties(rng):
    d = setup_inputs(rng)
    v = rng.standard_normal((128, 16, 12, 4), dtype=np.float32)
    v[:64, 1::2, 1::2] = v[:64, 1::2, ::2]
    s = rng.standard_normal((128, 16, 4), dtype=np.float32)
    s[64:, 1::2] = 0
    x = np.zeros((N, 128, 16, C, 4), np.float32)
    for b in range(16):
        own = np.stack([rng.permutation(N) < N // 2 for i in range(12)])
        own[1] = ~own[0]
        for r in range(N):
            e = rng.permutation(np.resize(np.flatnonzero(own[:, r]), C))
            x[r][:, b] = v[:, b][:, e]
    d["x"] = mx_ref.flush(x.reshape(N, 128, 4 * P).astype(BF))
    d["seed"] = same(mx_ref.flush(s.reshape(128, 64).astype(BF)))
    return d
def check_inputs(d):
    b = []
    for k in ("x", "seed", "w"):
        v = np.abs(d[k].astype(np.float32))
        if not (np.isfinite(v).all() and ((v == 0) | (v >= 2.0 ** -30) & (v <= 2.0 ** 30)).all()): b.append("a value of " + k)
    s = d["seed"].astype(np.float32)
    if not (s == s[:1]).all(): b.append("seed isn't the same on all ranks")
    return b
def reference(x, seed, w):
    q = [mx_ref.quantize(np.ascontiguousarray(x[r])) for r in range(N)]
    every = join(*q)
    c = mx_ref.quantize(np.ascontiguousarray(seed[0]))
    won, nb = [], np.zeros((R, 16), np.float32)
    for t in range(R):
        k = pick(c, np.concatenate([np.arange(16), np.full(112, -1)]))
        s = np.concatenate([mx_ref.matmul(k, v)[:16] for v in q], axis=1)
        s = s[CLOUD, np.arange(N * P)] + np.float32(0)
        m = s if t == 0 else np.maximum(m, s)
        e = []
        for b in range(16):
            i = np.flatnonzero(CLOUD == b)
            e.append(int(i[np.argmin(m[i])]))
        c = pick(every, np.array(e))
        won.append(c)
        nb[t] = e
    u = join(*won)
    oc, osc = emit(u)
    y = np.stack([np.concatenate([mx_ref.matmul(mx_ref.quantize(np.ascontiguousarray(cut(w[r], o))), u) for o in range(O)], axis=1) for r in range(N)])
    return {"oc": same(oc), "osc": same(osc), "nb": same(nb), "y": y}

@@ -1,0 +1,492 @@
+from concourse.bass import DstId, RemoteDMATransfer
+from concourse.mybir import dt, AluOpType, AxisListType, ActivationFunctionType
+
+R, P, O, N = 4, 1024, 2, 8
+HEAD = 64
+ZERO = 128
+F8 = "float8_e4m3fn_x4"
+SCRATCH = {
+    "xb": ("sbuf", [128, 4 * P], "bfloat16"),
+    "wb": ("sbuf", [128, 512 * O], "bfloat16"),
+    "sd": ("sbuf", [128, 576], "bfloat16"),
+    "wq": ("sbuf", [128, 128 * O], F8), "wp": ("sbuf", [128, 128 * O], "uint8"),
+    "ip": ("sbuf", [128, 8], "int32"),
+    "q32": ("sbuf", [128, 32], "float32"),
+    "j4": ("sbuf", [128, 256], "float32"),
+    "ja": ("sbuf", [128, 256], "float32"),
+    "c4": ("sbuf", [128, 4], "float32"),
+    "c8": ("sbuf", [128, 4], "float32"),
+    "cf": ("sbuf", [128, 16], "float32"),
+    "cl": ("sbuf", [128, 32], "uint16"),
+    "sg": ("sbuf", [128, 256 * (R + 1)], "bfloat16"),
+    "sh": ("sbuf", [128, 8 * (R + 1)], "bfloat16"),
+    "ct": ("sbuf", [128, 8], "float32"),
+    "ns": ("sbuf", [128, 8], "float32"),
+    "tmp": ("sbuf", [128, 256], "float32"),
+    "ofs": ("sbuf", [128, 32], "uint16"),
+    "nl": ("sbuf", [128, 32], "uint16"),
+    "res": ("sbuf", [128, 4], "float32"),
+    "resl": ("sbuf", [128, 4], "float32"),
+    "ysb": ("sbuf", [128, 64 * O], "float32"),
+    "ps": ("psum", [128, 512], "float32"),
+}
+for _t in range(R + 1):
+    SCRATCH["xq%d" % _t] = ("sbuf", [128, HEAD + P], F8)
+    SCRATCH["xp%d" % _t] = ("sbuf", [128, HEAD + P], "uint8")
+    SCRATCH["dq%d" % _t] = ("sbuf", [128, ZERO + 16], F8)
+    SCRATCH["dp%d" % _t] = ("sbuf", [128, ZERO + 16], "uint8")
+    SCRATCH["mk%d" % _t] = ("sbuf", [128, 256], "float32")
+    if _t:
+        _m = N if _t == 1 else N // 2
+        SCRATCH["rn%d" % _t] = ("sbuf", [128, 256], "float32")
+        SCRATCH["cm%d" % _t] = ("sbuf", [128, 32], "uint16")
+        SCRATCH["wc%d" % _t] = ("sbuf", [128, 512], F8)
+        SCRATCH["ws%d" % _t] = ("sbuf", [128, 512], "uint8")
+        SCRATCH["pq%d" % _t] = ("sbuf", [128, 16], F8)
+        SCRATCH["pp%d" % _t] = ("sbuf", [128, 16], "uint8")
+        SCRATCH["mq%d" % _t] = ("sbuf", [128, ZERO + 16 * _m], F8)
+        SCRATCH["mp%d" % _t] = ("sbuf", [128, ZERO + 16 * _m], "uint8")
+        SCRATCH["qm%d" % _t] = ("sbuf", [128, 4 * _m], "float32")
+        SCRATCH["yo%d" % _t] = ("sbuf", [128, 4], "float32")
+        SCRATCH["ym%d" % _t] = ("sbuf", [128, 4], "float32")
+        SCRATCH["yn%d" % _t] = ("sbuf", [128, 4], "float32")
+for _k in range(6):
+    SCRATCH["py%d" % _k] = ("psum", [128, 512], "float32")
+SEMAPHORES = ["v", "s", "t", "ty", "iot", "iou", "ls", "ld_s", "ld_w", "st", "sty", "qn", "rs"]
+SEMAPHORES += ["ld%d" % q for q in range(5)] + ["wc%d" % q for q in range(4)] + ["ws%d" % q for q in range(4)]
+SEMAPHORES += [n + "%d" % t for t in range(1, R + 1) for n in ("ym", "yn", "yc", "ys", "qm", "qc", "qs", "dc", "ds")]
+
+FAR = 1e29
+OUT = 8192.0
+
+
+def rank_program(g, core, T, topo):
+    rank = T.rank_of(core)
+    if rank is None:
+        return
+    A = AluOpType
+    X = AxisListType.X
+    ACT = ActivationFunctionType
+    CP, ID = ACT.Copy, ACT.Identity
+    S = T.sem
+    chips, ranks_of = [], {}
+    for c in T.cores:
+        if topo.chip(c) not in ranks_of:
+            chips.append(topo.chip(c))
+            ranks_of[topo.chip(c)] = []
+        ranks_of[topo.chip(c)].append(c)
+    me = chips.index(topo.chip(core))
+    ab = ranks_of[chips[me]].index(core)
+    mate = ranks_of[chips[me]][1 - ab]
+    nch = len(chips)
+    others = [chips[(me + k) % nch] for k in range(1, nch)]
+    peers = [ranks_of[h][ab] for h in others]
+
+    cnt = {"v": 0, "vw": 0, "s": 0, "sw": 0, "ty": 0, "ls": 0, "st": 0}
+
+    def V(call, after=None):
+        need = cnt["v"] if after is None else after
+        if cnt["vw"] < need:
+            g.vector.wait_ge(S.v, need)
+            cnt["vw"] = need
+        call().then_inc(S.v, 1)
+        cnt["v"] += 1
+        return cnt["v"]
+
+    def AC(call, after=0):
+        if cnt["sw"] < after:
+            g.scalar.wait_ge(S.s, after)
+            cnt["sw"] = after
+        call().then_inc(S.s, 1)
+        cnt["s"] += 1
+        return cnt["s"]
+
+    def bits(es):
+        return sum(1 << e for e in es)
+
+    def dst(c):
+        a = topo.addr(c)
+        return DstId(rid=a[0], pnc=a[1])
+
+    ES = topo.engines(core, peers[0])[:8]
+    EM = topo.engines(core, mate)[:16]
+    EO = [e for e in EM if e not in ES][:8]
+    MATE_INC = len(EM)
+    PEER_INC = 8
+    FLAT_INC = 16 + len(EO)
+    last_es = EO
+
+    def to_mate(out, in_, sem, es=None):
+        es = EM if es is None else es
+        rid, pid = topo.addr(mate)[:2]
+        g.remote_dma(out, in_, sem, S.ls, pid, rid, bits(es))
+        cnt["ls"] += len(es)
+
+    def fused(parts):
+        g.remote_dma_fused([RemoteDMATransfer(dst_ids=[dst(c)], dma_engine_mask=bits(e), remote_sem=sem, src=in_, dst=out)
+                            for c, e, out, in_, sem in parts], local_sem=S.ls)
+        cnt["ls"] += sum(len(p[1]) for p in parts)
+
+    def cuts(turn):
+        return [ES[0:4], ES[4:6], ES[6:8]] if turn == 0 else [ES[4:8], ES[0:2], ES[2:4]]
+
+    def to_peers(out, in_, sem, turn):
+        fused([(c, e, out, in_, sem) for c, e in zip(peers, cuts(turn))])
+
+    def to_roots(out, in_, sem, turn):
+        roots = [ranks_of[h][0] for h in others]
+        parts = [(c, e, out, in_, sem) for c, e in zip(roots, cuts(turn))]
+        fused(parts if ab == 0 else parts + [(mate, EO, out, in_, sem)])
+
+    def u8(ap):
+        return ap.bitcast(dt.uint8)
+
+    def u32(ap):
+        return ap.bitcast(dt.uint32)
+
+    tcol = [0]
+
+    def tmp(n=1):
+        a = tcol[0]
+        tcol[0] += n
+        return T.tmp[:, a:a + n]
+
+    vec = g.vector
+    act = g.scalar.activation
+    cols = [(0, 256), (256, 256), (512, 256), (768, 128), (896, 128)]
+    g.sync.dma_start(T.sd[:, 512:576], T.seed[:]).then_inc(S.ld_s, 16)
+    for k in range(5):
+        a, n = cols[k]
+        queue = g.sync if k % 2 == 0 else g.scalar
+        queue.dma_start(T.xb[:, 4 * a:4 * (a + n)], T.x[:, 4 * a:4 * (a + n)]).then_inc(S["ld%d" % k], 16)
+    g.sync.wait_ge(S.ld3, 16)
+    g.sync.wait_ge(S.ld4, 16)
+    g.sync.dma_start(T.wb[:], T.w[:]).then_inc(S.ld_w, 16)
+
+    g.iota(T.ip[:, 0:1], [[0, 1]], 0, 1).then_inc(S.iot, 1)
+    g.iota(T.q32[:], [[1, 4], [0, 8]], 0, 0, allow_small_or_imprecise_dtypes=True).then_inc(S.iot, 1)
+    g.iota(T.j4[:], [[1, 4], [0, 64]], 0, 0, allow_small_or_imprecise_dtypes=True).then_inc(S.iou, 1)
+    g.iota(T.c4[:], [[-1, 4]], 0, 0, allow_small_or_imprecise_dtypes=True).then_inc(S.iou, 1)
+    g.iota(T.c8[:], [[-2, 4]], 0, 0, allow_small_or_imprecise_dtypes=True).then_inc(S.iou, 1)
+
+    def cf(k):
+        return T.cf[:, k:k + 1]
+
+    def zeros(name, t):
+        return V(lambda: vec.quantize_mx(T["%sq%d" % (name, t)][:, 0:ZERO], T["%sp%d" % (name, t)][:, 0:ZERO], T.sd[:, 0:512]), after=0)
+
+    V(lambda: vec.memset(T.sd[:, 0:512], 0.0))
+    vec.wait_ge(S.iot, 2)
+    V(lambda: vec.tensor_scalar(T.ip[:, 1:2], T.ip[:, 0:1], 15, None, A.bitwise_and), after=0)
+    V(lambda: vec.tensor_scalar(T.ip[:, 2:3], T.ip[:, 0:1], 2, 3, A.logical_shift_right, A.bitwise_and), after=0)
+    V(lambda: vec.tensor_scalar(T.ip[:, 3:4], T.ip[:, 0:1], 3, None, A.bitwise_and), after=0)
+    V(lambda: vec.tensor_scalar(T.ip[:, 4:5], T.ip[:, 0:1], 4, None, A.logical_shift_right), after=0)
+    V(lambda: vec.tensor_copy(T.cf[:, 0:4], T.ip[:, 1:5]))
+    fb, fq, fr, fg = cf(0), cf(1), cf(2), cf(3)
+    b128, base, bnum = cf(4), cf(6), cf(7)
+    V(lambda: vec.tensor_scalar(b128, fb, float(ZERO), None, A.add))
+    V(lambda: vec.tensor_scalar(T.cl[:], T.q32[:], fq, b128, A.is_equal, A.mult))
+    for u in range(1, R + 1):
+        if (u - 1) % 2 == ab:
+            V(lambda: vec.tensor_scalar(cf(8 + u), fg, float(u - 1), None, A.is_equal), after=0)
+    if ab == 0:
+        zeros("m", 1)
+    vec.wait_ge(S.ld_s, 16)
+    d0_done = V(lambda: vec.quantize_mx(T.dq0[:, 0:144], T.dp0[:, 0:144], T.sd[:, 0:576]), after=0)
+
+    def windows(t, q0, p0, lst, ready=None):
+        wc, ws = T["wc%d" % t], T["ws%d" % t]
+        for q in range(4):
+            a, b, c, d = 128 * q, 128 * q + 128, 8 * q, 8 * q + 8
+            vec.tensor_copy(u32(wc[:, a:b]), u32(q0).indirect(lst[:, c:d])).then_inc(S["wc%d" % q], 1)
+            if q < 3 or not ready:
+                act(ws[:, a:b], p0.indirect(lst[:, c:d]), CP).then_inc(S["ws%d" % q], 1)
+            else:
+                vec.wait_ge(*ready)
+                vec.tensor_copy(ws[:, a:b], p0.indirect(lst[:, c:d])).then_inc(S["ws%d" % q], 1)
+
+    vec.wait_ge(S.v, d0_done)
+    cnt["vw"] = cnt["v"]
+    g.scalar.wait_ge(S.v, d0_done)
+    windows(1, T.dq0[:, 0:144], T.dp0[:, 0:144], T.cl)
+
+    g.scalar.wait_ge(S.iou, 3)
+    AC(lambda: act(base, fq, ID, bias=float(HEAD), scale=256.0))
+    AC(lambda: act(bnum, fq, ID, bias=float(P * rank), scale=256.0))
+    sj = AC(lambda: act(T.ja[:], T.j4[:], ACT.Abs, bias=fr, scale=-1.0))
+    consts = AC(lambda: act(T.mk0[:], T.ja[:], ID, bias=-FAR, scale=2 * FAR), after=sj)
+
+    def quant_x(k, a, n):
+        return V(lambda: vec.quantize_mx(T["xq%d" % k][:, HEAD + a:HEAD + a + n], T["xp%d" % k][:, HEAD + a:HEAD + a + n],
+                                         T.xb[:, 4 * a:4 * (a + n)]), after=0)
+
+    xdone = []
+    for k in range(5):
+        vec.wait_ge(S["ld%d" % k], 16)
+        xdone.append(quant_x(0, *cols[k]))
+    xdone[3] = xdone[4]
+    vec.wait_ge(S.s, consts)
+    source = {1: 0, 2: 0, 3: 3, 4: 3} if ab == 0 else {1: 0, 2: 2, 3: 2, 4: 4}
+
+    def score(t):
+        for q in range(4):
+            if t == 1:
+                g.tensor.wait_ge(S.v, xdone[q])
+            g.tensor.wait_ge(S["wc%d" % q], t)
+            g.tensor.wait_ge(S["ws%d" % q], t)
+            a = HEAD + 256 * q
+            i = g.tensor.matmul_mx(T.ps[:, 0:256], T["wc%d" % t][:, 128 * q:128 * q + 128], T["ws%d" % t][:, 128 * q:128 * q + 128],
+                                   T.xq0[:, a:a + 256], T.xp0[:, a:a + 256], q == 0, q == 3)
+        i.then_inc(S.t, 1)
+
+    ydone, wdone, picked = {}, [0], {}
+
+    def products(t):
+        k = 2 * ((t - 1) % 3)
+        if t == 1:
+            g.tensor.wait_ge(S.v, wdone[0])
+        if t == 4:
+            g.tensor.wait_ge(S.s, ydone[1])
+        if t in picked:
+            g.tensor.wait_ge(S.v, picked[t][0])
+            g.tensor.wait_ge(S.s, picked[t][1])
+        for o in range(O):
+            g.tensor.matmul_mx(T["py%d" % (k + o)][:, 0:128], T.wq[:, 128 * o:128 * o + 128], T.wp[:, 128 * o:128 * o + 128],
+                               T["dq%d" % t][:, 16:144], T["dp%d" % t][:, 16:144], True, True).then_inc(S.ty, 1)
+            cnt["ty"] += 1
+        g.scalar.wait_ge(S.ty, cnt["ty"])
+        both = t == R and ab == 0
+        if both:
+            vec.wait_ge(S.ty, cnt["ty"])
+        for o in range(O):
+            out, in_ = T.ysb[:, 64 * o + 16 * (t - 1):64 * o + 16 * t], T["py%d" % (k + o)][:, 112:128]
+            if both and o == 1:
+                g.scalar.wait_ge(S.v, V(lambda: vec.tensor_copy(out, in_), after=0))
+            else:
+                ydone[t] = AC(lambda: act(out, in_, CP))
+
+    oh_acc, num_acc = [], []
+
+    def rows(buf, which):
+        for k in range(R):
+            if k % 2 == which:
+                g.sync.dma_start(T.nb[k:k + 1, :], buf[16 * k:16 * k + 16, 0:1]).then_inc(S.st, 16)
+                cnt["st"] += 16
+
+    def resolve():
+        pr, nf = tmp(4), tmp(4)
+        vec.wait_ge(S.qn, PEER_INC)
+        V(lambda: vec.tensor_copy(nf, T.nl[:, 0:32:8]))
+        V(lambda: vec.tensor_tensor(pr, oh_acc[0], nf, A.mult))
+        v = V(lambda: vec.tensor_reduce(T.res[:, 0:1], pr, X, A.add))
+        g.wait_ge(S.v, v)
+        to_mate(T.resl[:, 0:1], T.res[:, 0:1], S.rs)
+        return v
+
+    def store(t, codes, scales):
+        dq, dp = T["dq%d" % t], T["dp%d" % t]
+        g.sync.wait_ge(*codes)
+        g.sync.dma_start(T.oc[:, 64 * (t - 1):64 * t], u8(dq[:, 128:144])).then_inc(S.st, 16)
+        g.sync.wait_ge(*scales)
+        for k in range(4):
+            g.sync.dma_start(T.osc[4 * k:4 * k + 4, 16 * (t - 1):16 * t], dp[32 * k:32 * k + 4, 128:144]).then_inc(S.st, 16)
+        cnt["st"] += 80
+
+    def which_slot(t, ns):
+        oh = tmp(4)
+        if t == 1:
+            d, dd = tmp(4), tmp(4)
+            V(lambda: vec.tensor_scalar(d, T.c8[:], ns, 0.5, A.subtract, A.subtract), after=0)
+            V(lambda: vec.tensor_tensor(dd, d, d, A.mult))
+            V(lambda: vec.tensor_scalar(oh, dd, 1.0, cf(8 + t), A.is_lt, A.mult))
+        else:
+            V(lambda: vec.tensor_scalar(oh, T.c4[:], ns, cf(8 + t), A.is_equal, A.mult), after=0)
+        if not oh_acc:
+            oh_acc.append(oh)
+        else:
+            oh2 = tmp(4)
+            V(lambda: vec.tensor_tensor(oh2, oh, oh_acc[0], A.add))
+            oh_acc[0] = oh2
+
+    def numbers(t, e, ns, ct):
+        own, fl, df, oo = tmp(), tmp(), tmp(), tmp()
+        vo = V(lambda: vec.tensor_scalar(own, ct, -1.0, bnum, A.mult, A.add), after=0)
+        if t == 1:
+            V(lambda: vec.tensor_scalar(fl, ns, -float(2 * me + 1), cf(8 + t), A.is_equal, A.mult), after=0)
+        else:
+            V(lambda: vec.tensor_scalar(fl, e, -1.0 / OUT, cf(8 + t), A.mult, A.mult), after=0)
+        vec.wait_ge(S["yn%d" % t], MATE_INC)
+        V(lambda: vec.tensor_tensor(df, T["yn%d" % t][:, 0:1], own, A.subtract), after=vo)
+        if not num_acc:
+            num_acc.append(tmp())
+            V(lambda: vec.tensor_scalar(oo, own, cf(8 + t), None, A.mult), after=vo)
+            V(lambda: vec.tensor_scalar(num_acc[0], df, fl, oo, A.mult, A.add))
+        else:
+            nl = T.nl[:, 8 * me:8 * me + 1]
+            V(lambda: vec.tensor_scalar(oo, own, cf(8 + t), num_acc[0], A.mult, A.add), after=vo)
+            g.wait_ge(S.v, V(lambda: vec.tensor_scalar(nl, df, fl, oo, A.mult, A.add)))
+            to_peers(nl, nl, S.qn, 1)
+
+    later = []
+    for t in range(1, R + 1):
+        root, flat = (t - 1) % 2 == ab, t == 1
+        merge = root and not flat
+        n = "%d" % t
+        mk, qm, rn, ct = T["mk" + n], T["qm" + n], T["rn" + n], T.ct[:, t:t + 1]
+        slot = rank if flat else me
+        nslot = N if flat else nch
+        mq, mp = T["mq" + n], T["mp" + n]
+        score(t)
+        vec.wait_ge(S.t, t)
+        V(lambda: vec.tensor_tensor(mk[:], T["mk%d" % (t - 1)][:], T.ps[:, 0:256], A.max), after=0)
+        vr = V(lambda: vec.tensor_tensor_scan(rn[:], mk[:], mk[:], FAR, A.min, A.min))
+        low = rn[:, 255:256]
+        g.scalar.wait_ge(S.v, vr)
+        sct = AC(lambda: act(T.sg[:, 256 * t:256 * t + 256], rn[:], ACT.Sign, bias=low, scale=-1.0, accum_out=ct))
+        off = T.ofs[:, 4 * t:4 * t + 1]
+        sq, sp = T["xq%d" % source[t]], T["xp%d" % source[t]]
+        e = None
+        if merge:
+            e, eb = tmp(), tmp()
+            ym, low2 = T["ym" + n][:, 0:1], qm[:, 4 * slot:4 * slot + 1]
+            vec.wait_ge(S["ym" + n], MATE_INC)
+            ve = V(lambda: vec.tensor_scalar(e, ym, low, -OUT, A.is_lt if ab == 0 else A.is_le, A.mult), after=vr)
+            vm = V(lambda: vec.tensor_tensor(low2, ym, low, A.min), after=vr)
+            vb = V(lambda: vec.tensor_scalar(eb, e, base, None, A.add), after=ve)
+            g.wait_ge(S.v, vm)
+            to_peers(low2, low2, S["qm" + n], 0)
+            vec.wait_ge(S.s, sct)
+            vo = V(lambda: vec.tensor_scalar(off, eb, ct, fb, A.subtract, A.max), after=vb)
+            vec.wait_ge(S["yc" + n], MATE_INC)
+        else:
+            g.wait_ge(S.v, vr)
+            if flat:
+                to_roots(qm[:, 4 * slot:4 * slot + 1], low, S["qm" + n], 0)
+                if root:
+                    scp = AC(lambda: act(qm[:, 4 * slot:4 * slot + 1], low, CP))
+            else:
+                to_mate(T["ym" + n][:, 0:1], low, S["ym" + n])
+            vec.wait_ge(S.s, sct)
+            vo = V(lambda: vec.tensor_scalar(off, ct, -1.0, base, A.mult, A.add), after=vr)
+        if flat or root:
+            a = ZERO + 16 * slot
+            oq, op = mq[:, a:a + 16], mp[:, a:a + 16]
+        else:
+            oq, op = T["pq" + n][:, 0:16], T["pp" + n][:, 0:16]
+        vp = V(lambda: vec.tensor_copy(u32(oq), u32(sq[:, 0:HEAD + P]).indirect(off)), after=vo)
+        g.scalar.wait_ge(S.v, vo)
+        if merge:
+            g.scalar.wait_ge(S["ys" + n], MATE_INC)
+        own_s = AC(lambda: act(op, sp[:, 0:HEAD + P].indirect(off), CP))
+        g.wait_ge(S.v, vp)
+        if flat:
+            to_roots(u8(oq), u8(oq), S["qc" + n], 1)
+            g.wait_ge(S.s, own_s)
+            to_roots(op, op, S["qs" + n], 0)
+        elif root:
+            to_peers(u8(oq), u8(oq), S["qc" + n], 1)
+            g.wait_ge(S.s, own_s)
+            to_peers(op, op, S["qs" + n], 0)
+        else:
+            to_mate(u8(T["xq" + n][:, 0:16]), u8(oq), S["yc" + n])
+            g.wait_ge(S.s, own_s)
+            to_mate(T["xp" + n][:, 0:16], op, S["ys" + n])
+        if not root:
+            yo = T["yo" + n][:, 0:1]
+            g.wait_ge(S.v, V(lambda: vec.tensor_scalar(yo, ct, -1.0, bnum, A.mult, A.add), after=0))
+            to_mate(T["yn" + n][:, 0:1], yo, S["yn" + n])
+            if t < 3:
+                for u in range(1, R + 1):
+                    zeros("d", u)
+                zd = zeros("m", t + 1)
+                g.scalar.wait_ge(S.v, zd)
+            if t < R:
+                for c in cols:
+                    quant_x(source[t + 1], *c)
+            if t < 3:
+                vec.wait_ge(S.ld_w, 16)
+                wdone[0] = V(lambda: vec.quantize_mx(T.wq[:, 0:128 * O], T.wp[:, 0:128 * O], T.wb[:, 0:512 * O]), after=0)
+            for f in later:
+                f()
+            later = []
+            if t > 1:
+                products(t - 1)
+            if t == R:
+                g.sync.wait_ge(S.v, resolve())
+                rows(T.res, ab)
+            vec.wait_ge(S.v, cnt["v"])
+            cnt["vw"] = cnt["v"]
+        dq, dp = T["dq" + n], T["dp" + n]
+        es = last_es if t == R else EM
+        if root:
+            if t == R:
+                numbers(t, e, None, ct)
+            b = tcol[0] + nslot - 1
+            rm, rl = tmp(nslot), T.tmp[:, b:b + 1]
+            ns, o2f = T.ns[:, t:t + 1], tmp()
+            inc = FLAT_INC if flat else PEER_INC
+            vec.wait_ge(S["qm" + n], inc)
+            if flat:
+                vec.wait_ge(S.s, scp)
+            v = V(lambda: vec.tensor_tensor_scan(rm, qm[:, 0:4 * nslot:4], qm[:, 0:4 * nslot:4], FAR, A.min, A.min), after=vo)
+            g.scalar.wait_ge(S.v, v)
+            sns = AC(lambda: act(T.sh[:, 8 * t:8 * t + nslot], rm, ACT.Sign, bias=rl, scale=-1.0, accum_out=ns))
+            vec.wait_ge(S.s, sns)
+            off2, lst = T.ofs[:, 4 * t + 2:4 * t + 3], T["cm" + n]
+            vo = V(lambda: vec.tensor_scalar(off2, ns, -16.0, b128, A.mult, A.add), after=0)
+            vl = vo
+            if t < R:
+                vf = V(lambda: vec.tensor_scalar(o2f, ns, -16.0, b128, A.mult, A.add), after=0)
+                if not flat:
+                    vl = V(lambda: vec.tensor_scalar(lst[:], T.q32[:], fq, o2f, A.is_equal, A.mult), after=vf)
+            if t > 1:
+                products(t - 1)
+            vec.wait_ge(S["qc" + n], inc)
+            g.scalar.wait_ge(S["qs" + n], inc)
+            wid = ZERO + 16 * nslot
+            vp = V(lambda: vec.tensor_copy(u32(dq[:, 128:144]), u32(mq[:, 0:wid]).indirect(off2)), after=vo)
+            if flat:
+                vl = V(lambda: vec.tensor_scalar(lst[:], T.q32[:], fq, o2f, A.is_equal, A.mult), after=vf)
+            g.scalar.wait_ge(S.v, vo)
+            sp_ = AC(lambda: act(dp[:, 128:144], mp[:, 0:wid].indirect(off2), CP), after=sns)
+            picked[t] = (vp, sp_)
+            g.wait_ge(S.v, vp)
+            to_mate(u8(dq[:, 128:144]), u8(dq[:, 128:144]), S["dc" + n], es)
+            g.wait_ge(S.s, sp_)
+            to_mate(dp[:, 128:144], dp[:, 128:144], S["ds" + n])
+            if t < R:
+                vec.wait_ge(S.v, vl)
+                cnt["vw"] = max(cnt["vw"], vl)
+                g.scalar.wait_ge(S.v, vl)
+                windows(t + 1, mq[:, 0:wid], mp[:, 0:wid], lst, (S["qs" + n], inc))
+                later.append(lambda t=t, e=e, ns=ns, ct=ct: (numbers(t, e, ns, ct), which_slot(t, ns)))
+                g.sync.wait_ge(S.t, t + 1)
+            store(t, (S.v, vp), (S.s, sp_))
+            if t == R:
+                products(R)
+                which_slot(t, ns)
+        else:
+            if t < R:
+                vec.wait_ge(S["dc" + n], len(es))
+                g.scalar.wait_ge(S["ds" + n], MATE_INC)
+                windows(t + 1, dq[:, 0:144], dp[:, 0:144], T.cl, (S["ds" + n], MATE_INC))
+            else:
+                g.tensor.wait_ge(S["dc" + n], len(es))
+                g.tensor.wait_ge(S["ds" + n], MATE_INC)
+            store(t, (S["dc" + n], len(es)), (S["ds" + n], MATE_INC))
+            if t == R:
+                products(R)
+        if t == R:
+            g.scalar.wait_ge(S.s, cnt["s"])
+            g.scalar.dma_start(T.y[:], T.ysb[:]).then_inc(S.sty, 16)
+            v = resolve() if root else 0
+            g.sync.wait_ge(S.rs, MATE_INC)
+            rows(T.resl, 1 - ab)
+            if root:
+                g.sync.wait_ge(S.v, v)
+                rows(T.res, ab)
+    g.sync.wait_ge(S.st, cnt["st"])
+    g.scalar.wait_ge(S.sty, 16)
+    g.wait_ge(S.ls, cnt["ls"])
+    g.wait_ge(S.v, cnt["v"])
+    g.wait_ge(S.s, cnt["s"])

@@ -2,7 +2,8 @@ from concourse.bass import DstId, RemoteDMATransfer
 from concourse.mybir import dt, AluOpType, AxisListType, ActivationFunctionType
 
 R, P, O, N = 4, 1024, 2, 8
-HEAD = 64
+HEAD = 144
+FED = HEAD - 16
 ZERO = 128
 F8 = "float8_e4m3fn_x4"
 SCRATCH = {
@@ -11,17 +12,20 @@ SCRATCH = {
     "sd": ("sbuf", [128, 576], "bfloat16"),
     "wq": ("sbuf", [128, 128 * O], F8), "wp": ("sbuf", [128, 128 * O], "uint8"),
     "ip": ("sbuf", [128, 8], "int32"),
-    "q32": ("sbuf", [128, 32], "float32"),
+    "q8": ("sbuf", [128, 8], "float32"),
+    "kt": ("sbuf", [128, 16], "float32"),
+    "rm": ("sbuf", [128, 16 * (R + 1)], "float32"),
     "j4": ("sbuf", [128, 256], "float32"),
     "ja": ("sbuf", [128, 256], "float32"),
     "c4": ("sbuf", [128, 4], "float32"),
     "c8": ("sbuf", [128, 4], "float32"),
     "cf": ("sbuf", [128, 16], "float32"),
-    "cl": ("sbuf", [128, 32], "uint16"),
-    "sg": ("sbuf", [128, 256 * (R + 1)], "bfloat16"),
-    "sh": ("sbuf", [128, 8 * (R + 1)], "bfloat16"),
+    "cl": ("sbuf", [128, 8], "uint16"),
+    "sg": ("sbuf", [128, 128 * (R + 1)], "bfloat16"),
+    "sh": ("sbuf", [128, 16 * (R + 1)], "bfloat16"),
     "ct": ("sbuf", [128, 8], "float32"),
     "ns": ("sbuf", [128, 8], "float32"),
+    "ee": ("sbuf", [128, 8], "float32"),
     "tmp": ("sbuf", [128, 256], "float32"),
     "ofs": ("sbuf", [128, 32], "uint16"),
     "nl": ("sbuf", [128, 32], "uint16"),
@@ -38,10 +42,10 @@ for _t in range(R + 1):
     SCRATCH["mk%d" % _t] = ("sbuf", [128, 256], "float32")
     if _t:
         _m = N if _t == 1 else N // 2
-        SCRATCH["rn%d" % _t] = ("sbuf", [128, 256], "float32")
-        SCRATCH["cm%d" % _t] = ("sbuf", [128, 32], "uint16")
-        SCRATCH["wc%d" % _t] = ("sbuf", [128, 512], F8)
-        SCRATCH["ws%d" % _t] = ("sbuf", [128, 512], "uint8")
+        SCRATCH["rn%d" % _t] = ("sbuf", [128, 128], "float32")
+        SCRATCH["cm%d" % _t] = ("sbuf", [128, 16], "uint16")
+        SCRATCH["wc%d" % _t] = ("sbuf", [128, 256], F8)
+        SCRATCH["ws%d" % _t] = ("sbuf", [128, 256], "uint8")
         SCRATCH["pq%d" % _t] = ("sbuf", [128, 16], F8)
         SCRATCH["pp%d" % _t] = ("sbuf", [128, 16], "uint8")
         SCRATCH["mq%d" % _t] = ("sbuf", [128, ZERO + 16 * _m], F8)
@@ -53,11 +57,10 @@ for _t in range(R + 1):
 for _k in range(6):
     SCRATCH["py%d" % _k] = ("psum", [128, 512], "float32")
 SEMAPHORES = ["v", "s", "t", "ty", "iot", "iou", "ls", "ld_s", "ld_w", "st", "sty", "qn", "rs"]
-SEMAPHORES += ["ld%d" % q for q in range(5)] + ["wc%d" % q for q in range(4)] + ["ws%d" % q for q in range(4)]
+SEMAPHORES += ["ld%d" % q for q in range(5)] + ["wc", "ws"]
 SEMAPHORES += [n + "%d" % t for t in range(1, R + 1) for n in ("ym", "yn", "yc", "ys", "qm", "qc", "qs", "dc", "ds")]
 
 FAR = 1e29
-OUT = 8192.0
 
 
 def rank_program(g, core, T, topo):
@@ -112,8 +115,8 @@ def rank_program(g, core, T, topo):
     EM = topo.engines(core, mate)[:16]
     EO = [e for e in EM if e not in ES][:8]
     MATE_INC = len(EM)
-    PEER_INC = 8
-    FLAT_INC = 16 + len(EO)
+    PEER_INC = len(ES) * len(peers)
+    FLAT_INC = 2 * PEER_INC + len(EO)
     last_es = EO
 
     def to_mate(out, in_, sem, es=None):
@@ -123,20 +126,17 @@ def rank_program(g, core, T, topo):
         cnt["ls"] += len(es)
 
     def fused(parts):
-        g.remote_dma_fused([RemoteDMATransfer(dst_ids=[dst(c)], dma_engine_mask=bits(e), remote_sem=sem, src=in_, dst=out)
-                            for c, e, out, in_, sem in parts], local_sem=S.ls)
+        g.remote_dma_fused([RemoteDMATransfer(dst_ids=[dst(c) for c in cs], dma_engine_mask=bits(e), remote_sem=sem,
+                                              srcs=[in_], dsts=[out] * len(cs))
+                            for cs, e, out, in_, sem in parts], local_sem=S.ls)
         cnt["ls"] += sum(len(p[1]) for p in parts)
 
-    def cuts(turn):
-        return [ES[0:4], ES[4:6], ES[6:8]] if turn == 0 else [ES[4:8], ES[0:2], ES[2:4]]
+    def to_peers(out, in_, sem):
+        fused([(peers, ES, out, in_, sem)])
 
-    def to_peers(out, in_, sem, turn):
-        fused([(c, e, out, in_, sem) for c, e in zip(peers, cuts(turn))])
-
-    def to_roots(out, in_, sem, turn):
-        roots = [ranks_of[h][0] for h in others]
-        parts = [(c, e, out, in_, sem) for c, e in zip(roots, cuts(turn))]
-        fused(parts if ab == 0 else parts + [(mate, EO, out, in_, sem)])
+    def to_roots(out, in_, sem):
+        parts = [([ranks_of[h][0] for h in others], ES, out, in_, sem)]
+        fused(parts if ab == 0 else parts + [([mate], EO, out, in_, sem)])
 
     def u8(ap):
         return ap.bitcast(dt.uint8)
@@ -157,53 +157,63 @@ def rank_program(g, core, T, topo):
     g.sync.dma_start(T.sd[:, 512:576], T.seed[:]).then_inc(S.ld_s, 16)
     for k in range(5):
         a, n = cols[k]
-        queue = g.sync if k % 2 == 0 else g.scalar
+        queue = g.scalar if k % 2 == 0 else g.sync
         queue.dma_start(T.xb[:, 4 * a:4 * (a + n)], T.x[:, 4 * a:4 * (a + n)]).then_inc(S["ld%d" % k], 16)
     g.sync.wait_ge(S.ld3, 16)
     g.sync.wait_ge(S.ld4, 16)
     g.sync.dma_start(T.wb[:], T.w[:]).then_inc(S.ld_w, 16)
 
     g.iota(T.ip[:, 0:1], [[0, 1]], 0, 1).then_inc(S.iot, 1)
-    g.iota(T.q32[:], [[1, 4], [0, 8]], 0, 0, allow_small_or_imprecise_dtypes=True).then_inc(S.iot, 1)
+    g.iota(T.q8[:], [[1, 4], [0, 2]], 0, 0, allow_small_or_imprecise_dtypes=True).then_inc(S.iot, 1)
     g.iota(T.j4[:], [[1, 4], [0, 64]], 0, 0, allow_small_or_imprecise_dtypes=True).then_inc(S.iou, 1)
-    g.iota(T.c4[:], [[-1, 4]], 0, 0, allow_small_or_imprecise_dtypes=True).then_inc(S.iou, 1)
-    g.iota(T.c8[:], [[-2, 4]], 0, 0, allow_small_or_imprecise_dtypes=True).then_inc(S.iou, 1)
+    g.iota(T.c4[:], [[-1, 4]], -1, 0, allow_small_or_imprecise_dtypes=True).then_inc(S.iou, 1)
+    g.iota(T.c8[:], [[-2, 4]], -1, 0, allow_small_or_imprecise_dtypes=True).then_inc(S.iou, 1)
 
     def cf(k):
         return T.cf[:, k:k + 1]
 
+    def lo(buf, k):
+        return buf[0:32, k:k + 1]
+
     def zeros(name, t):
+        if name == "w":
+            return V(lambda: vec.quantize_mx(T["wc%d" % t][:, 128:256], T["ws%d" % t][:, 128:256], T.sd[:, 0:512]), after=0)
         return V(lambda: vec.quantize_mx(T["%sq%d" % (name, t)][:, 0:ZERO], T["%sp%d" % (name, t)][:, 0:ZERO], T.sd[:, 0:512]), after=0)
 
+    def spread(call, after):
+        for k in range(4):
+            v = V(lambda: call(32 * k, 32 * k + 32), after=after)
+        return v
+
     V(lambda: vec.memset(T.sd[:, 0:512], 0.0))
+    V(lambda: vec.memset(T.rm[:], FAR), after=0)
+    V(lambda: vec.memset(T.kt[:, 8:16], -16.0), after=0)
     vec.wait_ge(S.iot, 2)
     V(lambda: vec.tensor_scalar(T.ip[:, 1:2], T.ip[:, 0:1], 15, None, A.bitwise_and), after=0)
     V(lambda: vec.tensor_scalar(T.ip[:, 2:3], T.ip[:, 0:1], 2, 3, A.logical_shift_right, A.bitwise_and), after=0)
     V(lambda: vec.tensor_scalar(T.ip[:, 3:4], T.ip[:, 0:1], 3, None, A.bitwise_and), after=0)
     V(lambda: vec.tensor_scalar(T.ip[:, 4:5], T.ip[:, 0:1], 4, None, A.logical_shift_right), after=0)
-    V(lambda: vec.tensor_copy(T.cf[:, 0:4], T.ip[:, 1:5]))
-    fb, fq, fr, fg = cf(0), cf(1), cf(2), cf(3)
-    b128, base, bnum = cf(4), cf(6), cf(7)
+    V(lambda: vec.tensor_scalar(T.ip[:, 5:6], T.ip[:, 0:1], 1, 7, A.logical_shift_right, A.bitwise_and), after=0)
+    V(lambda: vec.tensor_copy(T.cf[:, 0:5], T.ip[:, 1:6]))
+    fb, fq, fr, fg, fh = cf(0), cf(1), cf(2), cf(3), cf(4)
+    BASE, B112, BFED = 6, 13, 14
+    b128, base, bnum = cf(5), cf(BASE), cf(7)
     V(lambda: vec.tensor_scalar(b128, fb, float(ZERO), None, A.add))
-    V(lambda: vec.tensor_scalar(T.cl[:], T.q32[:], fq, b128, A.is_equal, A.mult))
+    V(lambda: vec.tensor_scalar(T.kt[:, 0:8], T.q8[:], fq, -16.0, A.is_equal, A.mult), after=0)
     for u in range(1, R + 1):
         if (u - 1) % 2 == ab:
-            V(lambda: vec.tensor_scalar(cf(8 + u), fg, float(u - 1), None, A.is_equal), after=0)
+            V(lambda: vec.tensor_scalar(cf(8 + u), fg, float((u - 1) // 2), None, A.is_equal), after=0)
+    V(lambda: vec.tensor_scalar(T.cl[:], T.q8[:], fq, b128, A.is_equal, A.mult))
+    zeros("w", 1)
+    zeros("w", 2)
     if ab == 0:
         zeros("m", 1)
     vec.wait_ge(S.ld_s, 16)
     d0_done = V(lambda: vec.quantize_mx(T.dq0[:, 0:144], T.dp0[:, 0:144], T.sd[:, 0:576]), after=0)
 
-    def windows(t, q0, p0, lst, ready=None):
-        wc, ws = T["wc%d" % t], T["ws%d" % t]
-        for q in range(4):
-            a, b, c, d = 128 * q, 128 * q + 128, 8 * q, 8 * q + 8
-            vec.tensor_copy(u32(wc[:, a:b]), u32(q0).indirect(lst[:, c:d])).then_inc(S["wc%d" % q], 1)
-            if q < 3 or not ready:
-                act(ws[:, a:b], p0.indirect(lst[:, c:d]), CP).then_inc(S["ws%d" % q], 1)
-            else:
-                vec.wait_ge(*ready)
-                vec.tensor_copy(ws[:, a:b], p0.indirect(lst[:, c:d])).then_inc(S["ws%d" % q], 1)
+    def windows(t, q0, p0, lst):
+        vec.tensor_copy(u32(T["wc%d" % t][:, 0:128]), u32(q0).indirect(lst[:, 0:8])).then_inc(S.wc, 1)
+        act(T["ws%d" % t][:, 0:128], p0.indirect(lst[:, 0:8]), CP).then_inc(S.ws, 1)
 
     vec.wait_ge(S.v, d0_done)
     cnt["vw"] = cnt["v"]
@@ -211,8 +221,10 @@ def rank_program(g, core, T, topo):
     windows(1, T.dq0[:, 0:144], T.dp0[:, 0:144], T.cl)
 
     g.scalar.wait_ge(S.iou, 3)
-    AC(lambda: act(base, fq, ID, bias=float(HEAD), scale=256.0))
-    AC(lambda: act(bnum, fq, ID, bias=float(P * rank), scale=256.0))
+    AC(lambda: act(base, fh, ID, bias=float(HEAD), scale=128.0))
+    AC(lambda: act(bnum, fh, ID, bias=float(P * rank), scale=128.0))
+    AC(lambda: act(cf(B112), fb, ID, bias=float(ZERO - 16), scale=1.0))
+    AC(lambda: act(cf(BFED), fb, ID, bias=float(FED), scale=1.0))
     sj = AC(lambda: act(T.ja[:], T.j4[:], ACT.Abs, bias=fr, scale=-1.0))
     consts = AC(lambda: act(T.mk0[:], T.ja[:], ID, bias=-FAR, scale=2 * FAR), after=sj)
 
@@ -229,13 +241,13 @@ def rank_program(g, core, T, topo):
     source = {1: 0, 2: 0, 3: 3, 4: 3} if ab == 0 else {1: 0, 2: 2, 3: 2, 4: 4}
 
     def score(t):
+        g.tensor.wait_ge(S.wc, t)
+        g.tensor.wait_ge(S.ws, t)
         for q in range(4):
             if t == 1:
                 g.tensor.wait_ge(S.v, xdone[q])
-            g.tensor.wait_ge(S["wc%d" % q], t)
-            g.tensor.wait_ge(S["ws%d" % q], t)
             a = HEAD + 256 * q
-            i = g.tensor.matmul_mx(T.ps[:, 0:256], T["wc%d" % t][:, 128 * q:128 * q + 128], T["ws%d" % t][:, 128 * q:128 * q + 128],
+            i = g.tensor.matmul_mx(T.ps[:, 0:256], T["wc%d" % t][:, 32 * q:32 * q + 128], T["ws%d" % t][:, 32 * q:32 * q + 128],
                                    T.xq0[:, a:a + 256], T.xp0[:, a:a + 256], q == 0, q == 3)
         i.then_inc(S.t, 1)
 
@@ -270,7 +282,7 @@ def rank_program(g, core, T, topo):
     def rows(buf, which):
         for k in range(R):
             if k % 2 == which:
-                g.sync.dma_start(T.nb[k:k + 1, :], buf[16 * k:16 * k + 16, 0:1]).then_inc(S.st, 16)
+                g.sync.dma_start(T.nb[k:k + 1, :], buf[16 * (k // 2):16 * (k // 2) + 16, 0:1]).then_inc(S.st, 16)
                 cnt["st"] += 16
 
     def resolve():
@@ -312,9 +324,9 @@ def rank_program(g, core, T, topo):
         own, fl, df, oo = tmp(), tmp(), tmp(), tmp()
         vo = V(lambda: vec.tensor_scalar(own, ct, -1.0, bnum, A.mult, A.add), after=0)
         if t == 1:
-            V(lambda: vec.tensor_scalar(fl, ns, -float(2 * me + 1), cf(8 + t), A.is_equal, A.mult), after=0)
+            V(lambda: vec.tensor_scalar(fl, ns, -float(2 * me + 2), cf(8 + t), A.is_equal, A.mult), after=0)
         else:
-            V(lambda: vec.tensor_scalar(fl, e, -1.0 / OUT, cf(8 + t), A.mult, A.mult), after=0)
+            V(lambda: vec.tensor_scalar(fl, e, 0.0, cf(8 + t), A.is_equal, A.mult), after=0)
         vec.wait_ge(S["yn%d" % t], MATE_INC)
         V(lambda: vec.tensor_tensor(df, T["yn%d" % t][:, 0:1], own, A.subtract), after=vo)
         if not num_acc:
@@ -325,8 +337,10 @@ def rank_program(g, core, T, topo):
             nl = T.nl[:, 8 * me:8 * me + 1]
             V(lambda: vec.tensor_scalar(oo, own, cf(8 + t), num_acc[0], A.mult, A.add), after=vo)
             g.wait_ge(S.v, V(lambda: vec.tensor_scalar(nl, df, fl, oo, A.mult, A.add)))
-            to_peers(nl, nl, S.qn, 1)
+            to_peers(nl, nl, S.qn)
 
+    shadow = {1: [("d", 1), ("d", 2), ("w", 3), ("m", 2)], 3: [("d", 3), ("d", 4), ("w", 4)],
+              2: [("d", 1), ("d", 2), ("d", 3), ("d", 4), ("w", 3), ("w", 4), ("m", 3)]}
     later = []
     for t in range(1, R + 1):
         root, flat = (t - 1) % 2 == ab, t == 1
@@ -339,35 +353,36 @@ def rank_program(g, core, T, topo):
         score(t)
         vec.wait_ge(S.t, t)
         V(lambda: vec.tensor_tensor(mk[:], T["mk%d" % (t - 1)][:], T.ps[:, 0:256], A.max), after=0)
-        vr = V(lambda: vec.tensor_tensor_scan(rn[:], mk[:], mk[:], FAR, A.min, A.min))
-        low = rn[:, 255:256]
+        vr = V(lambda: vec.tensor_tensor_scan(rn[:], mk[:, 0:128], mk[:, 128:256], FAR, A.min, A.min))
+        low = rn[:, 127:128]
         g.scalar.wait_ge(S.v, vr)
-        sct = AC(lambda: act(T.sg[:, 256 * t:256 * t + 256], rn[:], ACT.Sign, bias=low, scale=-1.0, accum_out=ct))
+        sct = AC(lambda: act(T.sg[:, 128 * t:128 * t + 128], rn[:], ACT.Sign, bias=low, scale=-1.0, accum_out=ct))
         off = T.ofs[:, 4 * t:4 * t + 1]
         sq, sp = T["xq%d" % source[t]], T["xp%d" % source[t]]
         e = None
         if merge:
-            e, eb = tmp(), tmp()
+            e = T.ee[:, t:t + 1]
             ym, low2 = T["ym" + n][:, 0:1], qm[:, 4 * slot:4 * slot + 1]
             vec.wait_ge(S["ym" + n], MATE_INC)
-            ve = V(lambda: vec.tensor_scalar(e, ym, low, -OUT, A.is_lt if ab == 0 else A.is_le, A.mult), after=vr)
             vm = V(lambda: vec.tensor_tensor(low2, ym, low, A.min), after=vr)
-            vb = V(lambda: vec.tensor_scalar(eb, e, base, None, A.add), after=ve)
+            ve = V(lambda: vec.tensor_scalar(e, ym, low, base, A.is_ge if ab == 0 else A.is_gt, A.mult), after=vr)
             g.wait_ge(S.v, vm)
-            to_peers(low2, low2, S["qm" + n], 0)
+            to_peers(low2, low2, S["qm" + n])
             vec.wait_ge(S.s, sct)
-            vo = V(lambda: vec.tensor_scalar(off, eb, ct, fb, A.subtract, A.max), after=vb)
+            vo = spread(lambda a, b: vec.tensor_scalar(T.ofs[a:b, 4 * t:4 * t + 1], lo(T.ee, t), lo(T.ct, t), lo(T.cf, BFED),
+                                                       A.subtract, A.max), ve)
             vec.wait_ge(S["yc" + n], MATE_INC)
         else:
             g.wait_ge(S.v, vr)
             if flat:
-                to_roots(qm[:, 4 * slot:4 * slot + 1], low, S["qm" + n], 0)
+                to_roots(qm[:, 4 * slot:4 * slot + 1], low, S["qm" + n])
                 if root:
                     scp = AC(lambda: act(qm[:, 4 * slot:4 * slot + 1], low, CP))
             else:
                 to_mate(T["ym" + n][:, 0:1], low, S["ym" + n])
             vec.wait_ge(S.s, sct)
-            vo = V(lambda: vec.tensor_scalar(off, ct, -1.0, base, A.mult, A.add), after=vr)
+            vo = spread(lambda a, b: vec.tensor_scalar(T.ofs[a:b, 4 * t:4 * t + 1], lo(T.ct, t), -1.0, lo(T.cf, BASE),
+                                                       A.mult, A.add), vr)
         if flat or root:
             a = ZERO + 16 * slot
             oq, op = mq[:, a:a + 16], mp[:, a:a + 16]
@@ -380,27 +395,25 @@ def rank_program(g, core, T, topo):
         own_s = AC(lambda: act(op, sp[:, 0:HEAD + P].indirect(off), CP))
         g.wait_ge(S.v, vp)
         if flat:
-            to_roots(u8(oq), u8(oq), S["qc" + n], 1)
+            to_roots(u8(oq), u8(oq), S["qc" + n])
             g.wait_ge(S.s, own_s)
-            to_roots(op, op, S["qs" + n], 0)
+            to_roots(op, op, S["qs" + n])
         elif root:
-            to_peers(u8(oq), u8(oq), S["qc" + n], 1)
+            to_peers(u8(oq), u8(oq), S["qc" + n])
             g.wait_ge(S.s, own_s)
-            to_peers(op, op, S["qs" + n], 0)
+            to_peers(op, op, S["qs" + n])
         else:
-            to_mate(u8(T["xq" + n][:, 0:16]), u8(oq), S["yc" + n])
+            to_mate(u8(T["xq" + n][:, FED:HEAD]), u8(oq), S["yc" + n])
             g.wait_ge(S.s, own_s)
-            to_mate(T["xp" + n][:, 0:16], op, S["ys" + n])
+            to_mate(T["xp" + n][:, FED:HEAD], op, S["ys" + n])
         if not root:
             yo = T["yo" + n][:, 0:1]
             g.wait_ge(S.v, V(lambda: vec.tensor_scalar(yo, ct, -1.0, bnum, A.mult, A.add), after=0))
             to_mate(T["yn" + n][:, 0:1], yo, S["yn" + n])
-            if t < 3:
-                for u in range(1, R + 1):
-                    zeros("d", u)
-                zd = zeros("m", t + 1)
-                g.scalar.wait_ge(S.v, zd)
             if t < R:
+                for name, u in shadow[t]:
+                    zd = zeros(name, u)
+                g.scalar.wait_ge(S.v, zd)
                 for c in cols:
                     quant_x(source[t + 1], *c)
             if t < 3:
@@ -410,6 +423,8 @@ def rank_program(g, core, T, topo):
                 f()
             later = []
             if t > 1:
+                g.sync.wait_ge(S.v, cnt["v"])
+                store(t - 1, (S.v, picked[t - 1][0]), (S.s, picked[t - 1][1]))
                 products(t - 1)
             if t == R:
                 g.sync.wait_ge(S.v, resolve())
@@ -421,32 +436,27 @@ def rank_program(g, core, T, topo):
         if root:
             if t == R:
                 numbers(t, e, None, ct)
-            b = tcol[0] + nslot - 1
-            rm, rl = tmp(nslot), T.tmp[:, b:b + 1]
-            ns, o2f = T.ns[:, t:t + 1], tmp()
+            a = 16 * t
+            rm, rl = T.rm[:, a + 1:a + 1 + nslot], T.rm[:, a + nslot:a + nslot + 1]
+            ns = T.ns[:, t:t + 1]
             inc = FLAT_INC if flat else PEER_INC
             vec.wait_ge(S["qm" + n], inc)
             if flat:
                 vec.wait_ge(S.s, scp)
             v = V(lambda: vec.tensor_tensor_scan(rm, qm[:, 0:4 * nslot:4], qm[:, 0:4 * nslot:4], FAR, A.min, A.min), after=vo)
             g.scalar.wait_ge(S.v, v)
-            sns = AC(lambda: act(T.sh[:, 8 * t:8 * t + nslot], rm, ACT.Sign, bias=rl, scale=-1.0, accum_out=ns))
+            sns = AC(lambda: act(T.sh[:, a:a + nslot + 1], T.rm[:, a:a + nslot + 1], ACT.Sign, bias=rl, scale=-1.0, accum_out=ns))
             vec.wait_ge(S.s, sns)
-            off2, lst = T.ofs[:, 4 * t + 2:4 * t + 3], T["cm" + n]
-            vo = V(lambda: vec.tensor_scalar(off2, ns, -16.0, b128, A.mult, A.add), after=0)
-            vl = vo
-            if t < R:
-                vf = V(lambda: vec.tensor_scalar(o2f, ns, -16.0, b128, A.mult, A.add), after=0)
-                if not flat:
-                    vl = V(lambda: vec.tensor_scalar(lst[:], T.q32[:], fq, o2f, A.is_equal, A.mult), after=vf)
+            lst = T["cm" + n]
+            off2 = lst[:, 8:9]
+            vo = spread(lambda a, b: vec.tensor_scalar(lst[a:b, 0:10], T.kt[0:32, 0:10], lo(T.ns, t), lo(T.cf, B112),
+                                                       A.mult, A.add), 0)
             if t > 1:
                 products(t - 1)
             vec.wait_ge(S["qc" + n], inc)
             g.scalar.wait_ge(S["qs" + n], inc)
             wid = ZERO + 16 * nslot
             vp = V(lambda: vec.tensor_copy(u32(dq[:, 128:144]), u32(mq[:, 0:wid]).indirect(off2)), after=vo)
-            if flat:
-                vl = V(lambda: vec.tensor_scalar(lst[:], T.q32[:], fq, o2f, A.is_equal, A.mult), after=vf)
             g.scalar.wait_ge(S.v, vo)
             sp_ = AC(lambda: act(dp[:, 128:144], mp[:, 0:wid].indirect(off2), CP), after=sns)
             picked[t] = (vp, sp_)
@@ -455,21 +465,17 @@ def rank_program(g, core, T, topo):
             g.wait_ge(S.s, sp_)
             to_mate(dp[:, 128:144], dp[:, 128:144], S["ds" + n])
             if t < R:
-                vec.wait_ge(S.v, vl)
-                cnt["vw"] = max(cnt["vw"], vl)
-                g.scalar.wait_ge(S.v, vl)
-                windows(t + 1, mq[:, 0:wid], mp[:, 0:wid], lst, (S["qs" + n], inc))
+                windows(t + 1, mq[:, 0:wid], mp[:, 0:wid], lst)
                 later.append(lambda t=t, e=e, ns=ns, ct=ct: (numbers(t, e, ns, ct), which_slot(t, ns)))
-                g.sync.wait_ge(S.t, t + 1)
-            store(t, (S.v, vp), (S.s, sp_))
-            if t == R:
+            else:
+                store(t, (S.v, vp), (S.s, sp_))
                 products(R)
                 which_slot(t, ns)
         else:
             if t < R:
                 vec.wait_ge(S["dc" + n], len(es))
                 g.scalar.wait_ge(S["ds" + n], MATE_INC)
-                windows(t + 1, dq[:, 0:144], dp[:, 0:144], T.cl, (S["ds" + n], MATE_INC))
+                windows(t + 1, dq[:, 0:144], dp[:, 0:144], T.cl)
             else:
                 g.tensor.wait_ge(S["dc" + n], len(es))
                 g.tensor.wait_ge(S["ds" + n], MATE_INC)

@@ -4,7 +4,9 @@ from concourse.mybir import dt, AluOpType, AxisListType, ActivationFunctionType
 R, P, O, N = 4, 1024, 2, 8
 HEAD = 144
 FED = HEAD - 16
-ZERO = 128
+ZERO = FED
+FLAT = (1, R)
+PIECES = [(0, 512), (512, 256), (768, 128), (896, 128)]
 F8 = "float8_e4m3fn_x4"
 SCRATCH = {
     "xb": ("sbuf", [128, 4 * P], "bfloat16"),
@@ -17,47 +19,51 @@ SCRATCH = {
     "rm": ("sbuf", [128, 16 * (R + 1)], "float32"),
     "j4": ("sbuf", [128, 256], "float32"),
     "ja": ("sbuf", [128, 256], "float32"),
-    "c4": ("sbuf", [128, 4], "float32"),
-    "c8": ("sbuf", [128, 4], "float32"),
+    "c8": ("sbuf", [128, 8], "float32"),
+    "k8": ("sbuf", [128, 8], "float32"),
+    "kv": ("sbuf", [128, 8], "float32"),
     "cf": ("sbuf", [128, 16], "float32"),
     "cl": ("sbuf", [128, 8], "uint16"),
     "sg": ("sbuf", [128, 128 * (R + 1)], "bfloat16"),
     "sh": ("sbuf", [128, 16 * (R + 1)], "bfloat16"),
     "ct": ("sbuf", [128, 8], "float32"),
+    "yo": ("sbuf", [128, 4 * R], "float32"),
     "ns": ("sbuf", [128, 8], "float32"),
     "ee": ("sbuf", [128, 8], "float32"),
-    "tmp": ("sbuf", [128, 256], "float32"),
+    "tmp": ("sbuf", [128, 64], "float32"),
     "ofs": ("sbuf", [128, 32], "uint16"),
-    "nl": ("sbuf", [128, 32], "uint16"),
     "res": ("sbuf", [128, 4], "float32"),
     "resl": ("sbuf", [128, 4], "float32"),
     "ysb": ("sbuf", [128, 64 * O], "float32"),
-    "ps": ("psum", [128, 512], "float32"),
+    "ps": ("psum", [128, 1024], "float32"),
 }
 for _t in range(R + 1):
-    SCRATCH["xq%d" % _t] = ("sbuf", [128, HEAD + P], F8)
-    SCRATCH["xp%d" % _t] = ("sbuf", [128, HEAD + P], "uint8")
+    if _t in (0, 2, 3):
+        SCRATCH["xq%d" % _t] = ("sbuf", [128, HEAD + P], F8)
+        SCRATCH["xp%d" % _t] = ("sbuf", [128, HEAD + P], "uint8")
     SCRATCH["dq%d" % _t] = ("sbuf", [128, ZERO + 16], F8)
     SCRATCH["dp%d" % _t] = ("sbuf", [128, ZERO + 16], "uint8")
     SCRATCH["mk%d" % _t] = ("sbuf", [128, 256], "float32")
     if _t:
-        _m = N if _t == 1 else N // 2
+        _m = N if _t in FLAT else N // 2
         SCRATCH["rn%d" % _t] = ("sbuf", [128, 128], "float32")
         SCRATCH["cm%d" % _t] = ("sbuf", [128, 16], "uint16")
-        SCRATCH["wc%d" % _t] = ("sbuf", [128, 256], F8)
-        SCRATCH["ws%d" % _t] = ("sbuf", [128, 256], "uint8")
-        SCRATCH["pq%d" % _t] = ("sbuf", [128, 16], F8)
-        SCRATCH["pp%d" % _t] = ("sbuf", [128, 16], "uint8")
         SCRATCH["mq%d" % _t] = ("sbuf", [128, ZERO + 16 * _m], F8)
         SCRATCH["mp%d" % _t] = ("sbuf", [128, ZERO + 16 * _m], "uint8")
         SCRATCH["qm%d" % _t] = ("sbuf", [128, 4 * _m], "float32")
-        SCRATCH["yo%d" % _t] = ("sbuf", [128, 4], "float32")
-        SCRATCH["ym%d" % _t] = ("sbuf", [128, 4], "float32")
+    if _t > 1:
+        SCRATCH["wc%d" % _t] = ("sbuf", [128, 256], F8)
+        SCRATCH["ws%d" % _t] = ("sbuf", [128, 256], "uint8")
+    if 0 < _t < R:
         SCRATCH["yn%d" % _t] = ("sbuf", [128, 4], "float32")
+    if 1 < _t < R:
+        SCRATCH["pq%d" % _t] = ("sbuf", [128, 16], F8)
+        SCRATCH["pp%d" % _t] = ("sbuf", [128, 16], "uint8")
+        SCRATCH["ym%d" % _t] = ("sbuf", [128, 4], "float32")
 for _k in range(6):
     SCRATCH["py%d" % _k] = ("psum", [128, 512], "float32")
-SEMAPHORES = ["v", "s", "t", "ty", "iot", "iou", "ls", "ld_s", "ld_w", "st", "sty", "qn", "rs"]
-SEMAPHORES += ["ld%d" % q for q in range(5)] + ["wc", "ws"]
+SEMAPHORES = ["v", "s", "t", "ty", "iot", "iou", "ls", "lw", "ld_s", "ld_w", "st", "sty", "rs", "wc", "ws"]
+SEMAPHORES += ["ld%d" % q for q in range(len(PIECES))]
 SEMAPHORES += [n + "%d" % t for t in range(1, R + 1) for n in ("ym", "yn", "yc", "ys", "qm", "qc", "qs", "dc", "ds")]
 
 FAR = 1e29
@@ -85,7 +91,7 @@ def rank_program(g, core, T, topo):
     others = [chips[(me + k) % nch] for k in range(1, nch)]
     peers = [ranks_of[h][ab] for h in others]
 
-    cnt = {"v": 0, "vw": 0, "s": 0, "sw": 0, "ty": 0, "ls": 0, "st": 0}
+    cnt = {"v": 0, "vw": 0, "s": 0, "sw": 0, "ty": 0, "ls": 0, "lw": 0, "st": 0, "sty": 0}
 
     def V(call, after=None):
         need = cnt["v"] if after is None else after
@@ -117,26 +123,25 @@ def rank_program(g, core, T, topo):
     MATE_INC = len(EM)
     PEER_INC = len(ES) * len(peers)
     FLAT_INC = 2 * PEER_INC + len(EO)
-    last_es = EO
 
-    def to_mate(out, in_, sem, es=None):
-        es = EM if es is None else es
+    def to_mate(out, in_, sem, left="ls"):
         rid, pid = topo.addr(mate)[:2]
-        g.remote_dma(out, in_, sem, S.ls, pid, rid, bits(es))
-        cnt["ls"] += len(es)
+        g.remote_dma(out, in_, sem, S[left], pid, rid, bits(EM))
+        cnt[left] += len(EM)
 
-    def fused(parts):
+    def fused(parts, left="ls"):
         g.remote_dma_fused([RemoteDMATransfer(dst_ids=[dst(c) for c in cs], dma_engine_mask=bits(e), remote_sem=sem,
                                               srcs=[in_], dsts=[out] * len(cs))
-                            for cs, e, out, in_, sem in parts], local_sem=S.ls)
-        cnt["ls"] += sum(len(p[1]) for p in parts)
+                            for cs, e, out, in_, sem in parts], local_sem=S[left])
+        cnt[left] += sum(len(p[1]) for p in parts)
 
     def to_peers(out, in_, sem):
         fused([(peers, ES, out, in_, sem)])
 
-    def to_roots(out, in_, sem):
-        parts = [([ranks_of[h][0] for h in others], ES, out, in_, sem)]
-        fused(parts if ab == 0 else parts + [([mate], EO, out, in_, sem)])
+    def to_roots(t, out, in_, sem, left="ls"):
+        who = (t - 1) % 2
+        parts = [([ranks_of[h][who] for h in others], ES, out, in_, sem)]
+        fused(parts if ab == who else parts + [([mate], EO, out, in_, sem)], left)
 
     def u8(ap):
         return ap.bitcast(dt.uint8)
@@ -149,31 +154,25 @@ def rank_program(g, core, T, topo):
     def tmp(n=1):
         a = tcol[0]
         tcol[0] += n
-        return T.tmp[:, a:a + n]
+        return T.tmp[0:32, a:a + n]
 
     vec = g.vector
     act = g.scalar.activation
-    cols = [(0, 256), (256, 256), (512, 256), (768, 128), (896, 128)]
-    g.sync.dma_start(T.sd[:, 512:576], T.seed[:]).then_inc(S.ld_s, 16)
-    for k in range(5):
-        a, n = cols[k]
-        queue = g.scalar if k % 2 == 0 else g.sync
-        queue.dma_start(T.xb[:, 4 * a:4 * (a + n)], T.x[:, 4 * a:4 * (a + n)]).then_inc(S["ld%d" % k], 16)
-    g.sync.wait_ge(S.ld3, 16)
-    g.sync.wait_ge(S.ld4, 16)
-    g.sync.dma_start(T.wb[:], T.w[:]).then_inc(S.ld_w, 16)
+    g.scalar.dma_start(T.sd[:, 512:576], T.seed[:]).then_inc(S.ld_s, 16)
+    for k, (a, n) in enumerate(PIECES):
+        g.scalar.dma_start(T.xb[:, 4 * a:4 * (a + n)], T.x[:, 4 * a:4 * (a + n)]).then_inc(S["ld%d" % k], 16)
 
-    g.iota(T.ip[:, 0:1], [[0, 1]], 0, 1).then_inc(S.iot, 1)
+    g.iota(T.ip[:, 0:1], [[0, 1]], ZERO, 1).then_inc(S.iot, 1)
     g.iota(T.q8[:], [[1, 4], [0, 2]], 0, 0, allow_small_or_imprecise_dtypes=True).then_inc(S.iot, 1)
     g.iota(T.j4[:], [[1, 4], [0, 64]], 0, 0, allow_small_or_imprecise_dtypes=True).then_inc(S.iou, 1)
-    g.iota(T.c4[:], [[-1, 4]], -1, 0, allow_small_or_imprecise_dtypes=True).then_inc(S.iou, 1)
-    g.iota(T.c8[:], [[-2, 4]], -1, 0, allow_small_or_imprecise_dtypes=True).then_inc(S.iou, 1)
+    g.iota(T.c8[:], [[-1, N]], -1, 0, allow_small_or_imprecise_dtypes=True).then_inc(S.iou, 1)
+    g.iota(T.k8[:], [[P, N]], -HEAD, 0, allow_small_or_imprecise_dtypes=True).then_inc(S.iou, 1)
 
     def cf(k):
         return T.cf[:, k:k + 1]
 
-    def lo(buf, k):
-        return buf[0:32, k:k + 1]
+    def lo(buf, k, run=0):
+        return buf[32 * run:32 * run + 32, k:k + 1]
 
     def zeros(name, t):
         if name == "w":
@@ -185,47 +184,46 @@ def rank_program(g, core, T, topo):
             v = V(lambda: call(32 * k, 32 * k + 32), after=after)
         return v
 
+    ql = T["qm%d" % R]
     V(lambda: vec.memset(T.sd[:, 0:512], 0.0))
-    V(lambda: vec.memset(T.rm[:], FAR), after=0)
-    V(lambda: vec.memset(T.kt[:, 8:16], -16.0), after=0)
     vec.wait_ge(S.iot, 2)
-    V(lambda: vec.tensor_scalar(T.ip[:, 1:2], T.ip[:, 0:1], 15, None, A.bitwise_and), after=0)
+    V(lambda: vec.tensor_scalar(T.ip[:, 1:2], T.ip[:, 0:1], ZERO + 15, None, A.bitwise_and), after=0)
     V(lambda: vec.tensor_scalar(T.ip[:, 2:3], T.ip[:, 0:1], 2, 3, A.logical_shift_right, A.bitwise_and), after=0)
     V(lambda: vec.tensor_scalar(T.ip[:, 3:4], T.ip[:, 0:1], 3, None, A.bitwise_and), after=0)
-    V(lambda: vec.tensor_scalar(T.ip[:, 4:5], T.ip[:, 0:1], 4, None, A.logical_shift_right), after=0)
-    V(lambda: vec.tensor_scalar(T.ip[:, 5:6], T.ip[:, 0:1], 1, 7, A.logical_shift_right, A.bitwise_and), after=0)
-    V(lambda: vec.tensor_copy(T.cf[:, 0:5], T.ip[:, 1:6]))
-    fb, fq, fr, fg, fh = cf(0), cf(1), cf(2), cf(3), cf(4)
-    BASE, B112, BFED = 6, 13, 14
-    b128, base, bnum = cf(5), cf(BASE), cf(7)
-    V(lambda: vec.tensor_scalar(b128, fb, float(ZERO), None, A.add))
-    V(lambda: vec.tensor_scalar(T.kt[:, 0:8], T.q8[:], fq, -16.0, A.is_equal, A.mult), after=0)
-    for u in range(1, R + 1):
-        if (u - 1) % 2 == ab:
-            V(lambda: vec.tensor_scalar(cf(8 + u), fg, float((u - 1) // 2), None, A.is_equal), after=0)
+    V(lambda: vec.tensor_scalar(T.ip[:, 4:5], T.ip[:, 0:1], 1, 7, A.logical_shift_right, A.bitwise_and), after=0)
+    V(lambda: vec.tensor_scalar(T.ip[:, 5:6], T.ip[:, 0:1], 4, 7, A.logical_shift_right, A.bitwise_and), after=0)
+    vc = V(lambda: vec.tensor_copy(T.cf[:, 0:5], T.ip[:, 1:6]))
+    b128, fq, fr, fh, fg = cf(0), cf(1), cf(2), cf(3), cf(4)
+    B128, BASE, BNUM, MINE, LAST, FIRST, B112 = 0, 6, 7, 8, 9, 10, 13
+    base, bnum = cf(BASE), cf(BNUM)
     V(lambda: vec.tensor_scalar(T.cl[:], T.q8[:], fq, b128, A.is_equal, A.mult))
-    zeros("w", 1)
-    zeros("w", 2)
-    if ab == 0:
-        zeros("m", 1)
     vec.wait_ge(S.ld_s, 16)
     d0_done = V(lambda: vec.quantize_mx(T.dq0[:, 0:144], T.dp0[:, 0:144], T.sd[:, 0:576]), after=0)
+    V(lambda: vec.tensor_copy(u32(T.xq0[:, 16:HEAD]), u32(T.dq0[:, 0:144]).indirect(T.cl[:, 0:8])))
 
-    def windows(t, q0, p0, lst):
-        vec.tensor_copy(u32(T["wc%d" % t][:, 0:128]), u32(q0).indirect(lst[:, 0:8])).then_inc(S.wc, 1)
-        act(T["ws%d" % t][:, 0:128], p0.indirect(lst[:, 0:8]), CP).then_inc(S.ws, 1)
+    def for_roots():
+        V(lambda: vec.memset(T.rm[:], FAR), after=0)
+        V(lambda: vec.memset(T.kt[:, 8:16], -16.0), after=0)
+        V(lambda: vec.tensor_scalar(T.kt[:, 0:8], T.q8[:], fq, -16.0, A.is_equal, A.mult), after=0)
+        zeros("w", 2)
 
-    vec.wait_ge(S.v, d0_done)
-    cnt["vw"] = cnt["v"]
-    g.scalar.wait_ge(S.v, d0_done)
-    windows(1, T.dq0[:, 0:144], T.dp0[:, 0:144], T.cl)
+    def windows(t, q0, p0, lst, scales):
+        wc, ws = T["wc%d" % t], T["ws%d" % t]
+        vec.tensor_copy(u32(wc[:, 96:128]), u32(q0).indirect(lst[:, 6:8])).then_inc(S.wc, 1)
+        vec.wait_ge(*scales)
+        vec.tensor_copy(ws[:, 96:128], p0.indirect(lst[:, 6:8])).then_inc(S.wc, 1)
+        vec.tensor_copy(u32(wc[:, 0:96]), u32(q0).indirect(lst[:, 0:6])).then_inc(S.wc, 1)
+        act(ws[:, 0:96], p0.indirect(lst[:, 0:6]), CP).then_inc(S.ws, 1)
 
-    g.scalar.wait_ge(S.iou, 3)
-    AC(lambda: act(base, fh, ID, bias=float(HEAD), scale=128.0))
+    g.scalar.wait_ge(S.v, vc)
+    sb = AC(lambda: act(base, fh, ID, bias=float(HEAD), scale=128.0))
     AC(lambda: act(bnum, fh, ID, bias=float(P * rank), scale=128.0))
-    AC(lambda: act(cf(B112), fb, ID, bias=float(ZERO - 16), scale=1.0))
-    AC(lambda: act(cf(BFED), fb, ID, bias=float(FED), scale=1.0))
+    AC(lambda: act(cf(B112), b128, ID, bias=-16.0, scale=1.0))
+    g.scalar.wait_ge(S.iou, 3)
     sj = AC(lambda: act(T.ja[:], T.j4[:], ACT.Abs, bias=fr, scale=-1.0))
+    g.scalar.wait_ge(S.v, d0_done)
+    s1_done = AC(lambda: act(T.xp0[:, 16:HEAD], T.dp0[:, 0:144].indirect(T.cl[:, 0:8]), CP))
+    AC(lambda: act(T.kv[:], T.k8[:], ID, bias=base, scale=1.0), after=sb)
     consts = AC(lambda: act(T.mk0[:], T.ja[:], ID, bias=-FAR, scale=2 * FAR), after=sj)
 
     def quant_x(k, a, n):
@@ -233,25 +231,41 @@ def rank_program(g, core, T, topo):
                                          T.xb[:, 4 * a:4 * (a + n)]), after=0)
 
     xdone = []
-    for k in range(5):
+    for k, (a, n) in enumerate(PIECES):
         vec.wait_ge(S["ld%d" % k], 16)
-        xdone.append(quant_x(0, *cols[k]))
-    xdone[3] = xdone[4]
+        xdone += [quant_x(0, a, n)] * (n // 128)
     vec.wait_ge(S.s, consts)
-    source = {1: 0, 2: 0, 3: 3, 4: 3} if ab == 0 else {1: 0, 2: 2, 3: 2, 4: 4}
+    source = {1: 0, 2: 0, 3: 3, 4: 3} if ab == 0 else {1: 0, 2: 2, 3: 2, 4: 2}
 
     def score(t):
-        g.tensor.wait_ge(S.wc, t)
-        g.tensor.wait_ge(S.ws, t)
-        for q in range(4):
+        if t == 1:
+            order = [(q, h) for q in range(4) for h in range(2)]
+            wc, ws = T.xq0, T.xp0
+            g.tensor.wait_ge(S.s, s1_done)
+        else:
+            order = [(3, 0), (3, 1), (2, 0), (1, 0), (0, 0), (2, 1), (1, 1), (0, 1)]
+            wc, ws = T["wc%d" % t], T["ws%d" % t]
+            g.tensor.wait_ge(S.wc, 3 * t - 4)
+        seen, rest = [0, 0], t == 1
+        for q, h in order:
+            if q < 3 and not rest:
+                g.tensor.wait_ge(S.wc, 3 * t - 3)
+                g.tensor.wait_ge(S.ws, t - 1)
+                rest = True
             if t == 1:
-                g.tensor.wait_ge(S.v, xdone[q])
-            a = HEAD + 256 * q
-            i = g.tensor.matmul_mx(T.ps[:, 0:256], T["wc%d" % t][:, 32 * q:32 * q + 128], T["ws%d" % t][:, 32 * q:32 * q + 128],
-                                   T.xq0[:, a:a + 256], T.xp0[:, a:a + 256], q == 0, q == 3)
-        i.then_inc(S.t, 1)
+                g.tensor.wait_ge(S.v, xdone[2 * q + h])
+            a, c = HEAD + 256 * q + 128 * h, 32 * q + (16 if t == 1 else 0)
+            seen[h] += 1
+            i = g.tensor.matmul_mx(T.ps[:, 512 * h:512 * h + 128], wc[:, c:c + 128], ws[:, c:c + 128],
+                                   T.xq0[:, a:a + 128], T.xp0[:, a:a + 128], seen[h] == 1, seen[h] == 4)
+            if seen[h] == 4:
+                i.then_inc(S.t, 1)
 
     ydone, wdone, picked = {}, [0], {}
+
+    def ystore(queue, a, b):
+        queue.dma_start(T.y[:, a:b], T.ysb[:, a:b]).then_inc(S.sty, 16)
+        cnt["sty"] += 16
 
     def products(t):
         k = 2 * ((t - 1) % 3)
@@ -266,33 +280,16 @@ def rank_program(g, core, T, topo):
             g.tensor.matmul_mx(T["py%d" % (k + o)][:, 0:128], T.wq[:, 128 * o:128 * o + 128], T.wp[:, 128 * o:128 * o + 128],
                                T["dq%d" % t][:, 16:144], T["dp%d" % t][:, 16:144], True, True).then_inc(S.ty, 1)
             cnt["ty"] += 1
-        g.scalar.wait_ge(S.ty, cnt["ty"])
         both = t == R and ab == 0
-        if both:
-            vec.wait_ge(S.ty, cnt["ty"])
+        v = 0
         for o in range(O):
             out, in_ = T.ysb[:, 64 * o + 16 * (t - 1):64 * o + 16 * t], T["py%d" % (k + o)][:, 112:128]
             if both and o == 1:
-                g.scalar.wait_ge(S.v, V(lambda: vec.tensor_copy(out, in_), after=0))
+                vec.wait_ge(S.ty, cnt["ty"])
+                v = V(lambda: vec.tensor_copy(out, in_), after=0)
             else:
+                g.scalar.wait_ge(S.ty, cnt["ty"] - O + 1 + o)
                 ydone[t] = AC(lambda: act(out, in_, CP))
-
-    oh_acc, num_acc = [], []
-
-    def rows(buf, which):
-        for k in range(R):
-            if k % 2 == which:
-                g.sync.dma_start(T.nb[k:k + 1, :], buf[16 * (k // 2):16 * (k // 2) + 16, 0:1]).then_inc(S.st, 16)
-                cnt["st"] += 16
-
-    def resolve():
-        pr, nf = tmp(4), tmp(4)
-        vec.wait_ge(S.qn, PEER_INC)
-        V(lambda: vec.tensor_copy(nf, T.nl[:, 0:32:8]))
-        V(lambda: vec.tensor_tensor(pr, oh_acc[0], nf, A.mult))
-        v = V(lambda: vec.tensor_reduce(T.res[:, 0:1], pr, X, A.add))
-        g.wait_ge(S.v, v)
-        to_mate(T.resl[:, 0:1], T.res[:, 0:1], S.rs)
         return v
 
     def store(t, codes, scales):
@@ -304,84 +301,92 @@ def rank_program(g, core, T, topo):
             g.sync.dma_start(T.osc[4 * k:4 * k + 4, 16 * (t - 1):16 * t], dp[32 * k:32 * k + 4, 128:144]).then_inc(S.st, 16)
         cnt["st"] += 80
 
-    def which_slot(t, ns):
-        oh = tmp(4)
-        if t == 1:
-            d, dd = tmp(4), tmp(4)
-            V(lambda: vec.tensor_scalar(d, T.c8[:], ns, 0.5, A.subtract, A.subtract), after=0)
-            V(lambda: vec.tensor_tensor(dd, d, d, A.mult))
-            V(lambda: vec.tensor_scalar(oh, dd, 1.0, cf(8 + t), A.is_lt, A.mult))
-        else:
-            V(lambda: vec.tensor_scalar(oh, T.c4[:], ns, cf(8 + t), A.is_equal, A.mult), after=0)
-        if not oh_acc:
-            oh_acc.append(oh)
-        else:
-            oh2 = tmp(4)
-            V(lambda: vec.tensor_tensor(oh2, oh, oh_acc[0], A.add))
-            oh_acc[0] = oh2
+    def store_nb(buf):
+        g.sync.dma_start(T.nb[:], buf[64:128, 0:1]).then_inc(S.st, 16)
+        cnt["st"] += 16
 
-    def numbers(t, e, ns, ct):
-        own, fl, df, oo = tmp(), tmp(), tmp(), tmp()
-        vo = V(lambda: vec.tensor_scalar(own, ct, -1.0, bnum, A.mult, A.add), after=0)
-        if t == 1:
-            V(lambda: vec.tensor_scalar(fl, ns, -float(2 * me + 2), cf(8 + t), A.is_equal, A.mult), after=0)
-        else:
-            V(lambda: vec.tensor_scalar(fl, e, 0.0, cf(8 + t), A.is_equal, A.mult), after=0)
+    def send_number(t, left="ls"):
+        v = V(lambda: vec.tensor_scalar(lo(T.yo, 4 * t), lo(T.ct, t), -1.0, lo(T.cf, BNUM), A.mult, A.add),
+              after=None if t == 1 else 0)
+        if t == 2:
+            v = V(lambda: vec.tensor_copy(lo(T.yo, 4 * t, 1), lo(T.ns, 1)), after=0)
+        g.wait_ge(S.v, v)
+        to_mate(T["yn%d" % t][:, 0:1], T.yo[:, 4 * t:4 * t + 1], S["yn%d" % t], left)
+
+    def numbers(t, out):
+        ns, ct, yn = lo(T.ns, t), lo(T.ct, t), lo(T["yn%d" % t], 0)
+        own, won, a, b = tmp(), tmp(), tmp(), tmp()
+        V(lambda: vec.tensor_scalar(own, ct, -1.0, lo(T.cf, BNUM), A.mult, A.add), after=0)
         vec.wait_ge(S["yn%d" % t], MATE_INC)
-        V(lambda: vec.tensor_tensor(df, T["yn%d" % t][:, 0:1], own, A.subtract), after=vo)
-        if not num_acc:
-            num_acc.append(tmp())
-            V(lambda: vec.tensor_scalar(oo, own, cf(8 + t), None, A.mult), after=vo)
-            V(lambda: vec.tensor_scalar(num_acc[0], df, fl, oo, A.mult, A.add))
-        else:
-            nl = T.nl[:, 8 * me:8 * me + 1]
-            V(lambda: vec.tensor_scalar(oo, own, cf(8 + t), num_acc[0], A.mult, A.add), after=vo)
-            g.wait_ge(S.v, V(lambda: vec.tensor_scalar(nl, df, fl, oo, A.mult, A.add)))
-            to_peers(nl, nl, S.qn)
+        if t in FLAT:
+            V(lambda: vec.tensor_scalar(won, lo(T.yn2, 0, 1), lo(T.cf, FIRST, 1), None, A.mult), after=0)
+            v = V(lambda: vec.tensor_scalar(a, won, -float(rank + 1), own, A.is_equal, A.mult))
+            V(lambda: vec.tensor_scalar(b, won, -float(T.rank_of(mate) + 1), yn, A.is_equal, A.mult), after=v - 1)
+            return V(lambda: vec.tensor_tensor(out, a, b, A.add))
+        V(lambda: vec.tensor_scalar(won, ns, -float(me + 1), lo(T.cf, MINE), A.is_equal, A.mult), after=0)
+        V(lambda: vec.tensor_tensor(a, yn, own, A.subtract), after=cnt["v"] - 1)
+        V(lambda: vec.tensor_scalar(b, lo(T.ee, t), 0.0, a, A.is_equal, A.mult))
+        return V(lambda: vec.tensor_scalar(out, b, own, won, A.add, A.mult))
 
-    shadow = {1: [("d", 1), ("d", 2), ("w", 3), ("m", 2)], 3: [("d", 3), ("d", 4), ("w", 4)],
+    def resolve():
+        val, oh = tmp(N), tmp(N)
+        V(lambda: vec.tensor_tensor(val, T.kv[0:32, :], ql[0:32, 0:4 * N:4], A.subtract), after=0)
+        V(lambda: vec.tensor_scalar(oh, T.c8[32:64, :], lo(T.ns, R, 1), lo(T.cf, LAST, 1), A.is_equal, A.mult), after=0)
+        V(lambda: vec.tensor_tensor(ql[96:128, 1:4 * N:4], oh, val, A.mult))
+        return V(lambda: vec.tensor_reduce(T.res[64:128, 0:1], ql[64:128, :], X, A.add))
+
+    shadow = {1: [("d", 1), ("w", 3), ("m", 2)], 3: [("d", 2), ("d", 3), ("d", 4), ("w", 4)],
               2: [("d", 1), ("d", 2), ("d", 3), ("d", 4), ("w", 3), ("w", 4), ("m", 3)]}
-    later = []
     for t in range(1, R + 1):
-        root, flat = (t - 1) % 2 == ab, t == 1
+        root, flat, last = (t - 1) % 2 == ab, t in FLAT, t == R
         merge = root and not flat
         n = "%d" % t
-        mk, qm, rn, ct = T["mk" + n], T["qm" + n], T["rn" + n], T.ct[:, t:t + 1]
+        mk, qm, rn = T["mk" + n], T["qm" + n], T["rn" + n]
         slot = rank if flat else me
         nslot = N if flat else nch
         mq, mp = T["mq" + n], T["mp" + n]
+        mine = qm[:, 4 * slot:4 * slot + 1]
         score(t)
-        vec.wait_ge(S.t, t)
-        V(lambda: vec.tensor_tensor(mk[:], T["mk%d" % (t - 1)][:], T.ps[:, 0:256], A.max), after=0)
+        for h in range(2):
+            vec.wait_ge(S.t, 2 * t - 1 + h)
+            V(lambda: vec.tensor_tensor(mk[:, 128 * h:128 * h + 128], T["mk%d" % (t - 1)][:, 128 * h:128 * h + 128],
+                                        T.ps[:, 512 * h:512 * h + 128], A.max), after=0)
         vr = V(lambda: vec.tensor_tensor_scan(rn[:], mk[:, 0:128], mk[:, 128:256], FAR, A.min, A.min))
         low = rn[:, 127:128]
         g.scalar.wait_ge(S.v, vr)
-        sct = AC(lambda: act(T.sg[:, 128 * t:128 * t + 128], rn[:], ACT.Sign, bias=low, scale=-1.0, accum_out=ct))
+        ct = lo(qm, 4 * slot) if last else lo(T.ct, t)
+        sct = AC(lambda: act(T.sg[0:32, 128 * t:128 * t + 128], rn[0:32, :], ACT.Sign, bias=lo(rn, 127), scale=-1.0,
+                             accum_out=ct))
         off = T.ofs[:, 4 * t:4 * t + 1]
         sq, sp = T["xq%d" % source[t]], T["xp%d" % source[t]]
-        e = None
         if merge:
-            e = T.ee[:, t:t + 1]
-            ym, low2 = T["ym" + n][:, 0:1], qm[:, 4 * slot:4 * slot + 1]
+            ym = T["ym" + n][:, 0:1]
             vec.wait_ge(S["ym" + n], MATE_INC)
-            vm = V(lambda: vec.tensor_tensor(low2, ym, low, A.min), after=vr)
-            ve = V(lambda: vec.tensor_scalar(e, ym, low, base, A.is_ge if ab == 0 else A.is_gt, A.mult), after=vr)
+            vm = V(lambda: vec.tensor_tensor(mine, ym, low, A.min), after=vr)
+            ve = V(lambda: vec.tensor_scalar(T.ee[:, t:t + 1], ym, low, base, A.is_ge if ab == 0 else A.is_gt, A.mult),
+                   after=vr)
             g.wait_ge(S.v, vm)
-            to_peers(low2, low2, S["qm" + n])
+            to_peers(mine, mine, S["qm" + n])
             vec.wait_ge(S.s, sct)
-            vo = spread(lambda a, b: vec.tensor_scalar(T.ofs[a:b, 4 * t:4 * t + 1], lo(T.ee, t), lo(T.ct, t), lo(T.cf, BFED),
+            vo = spread(lambda a, b: vec.tensor_scalar(T.ofs[a:b, 4 * t:4 * t + 1], lo(T.ee, t), ct, lo(T.cf, B128),
                                                        A.subtract, A.max), ve)
             vec.wait_ge(S["yc" + n], MATE_INC)
         else:
-            g.wait_ge(S.v, vr)
-            if flat:
-                to_roots(qm[:, 4 * slot:4 * slot + 1], low, S["qm" + n])
-                if root:
-                    scp = AC(lambda: act(qm[:, 4 * slot:4 * slot + 1], low, CP))
+            if last:
+                vm = V(lambda: vec.tensor_copy(lo(qm, 4 * slot, 1), lo(rn, 127)), after=vr)
+                g.wait_ge(S.v, vm)
+                g.wait_ge(S.s, sct)
+                to_roots(t, mine, mine, S["qm" + n])
             else:
-                to_mate(T["ym" + n][:, 0:1], low, S["ym" + n])
+                g.wait_ge(S.v, vr)
+                if flat:
+                    to_roots(t, mine, low, S["qm" + n])
+                    if root:
+                        scp = AC(lambda: act(mine, low, CP))
+                else:
+                    to_mate(T["ym" + n][:, 0:1], low, S["ym" + n])
             vec.wait_ge(S.s, sct)
-            vo = spread(lambda a, b: vec.tensor_scalar(T.ofs[a:b, 4 * t:4 * t + 1], lo(T.ct, t), -1.0, lo(T.cf, BASE),
+            vo = spread(lambda a, b: vec.tensor_scalar(T.ofs[a:b, 4 * t:4 * t + 1], ct, -1.0, lo(T.cf, BASE),
                                                        A.mult, A.add), vr)
         if flat or root:
             a = ZERO + 16 * slot
@@ -395,9 +400,9 @@ def rank_program(g, core, T, topo):
         own_s = AC(lambda: act(op, sp[:, 0:HEAD + P].indirect(off), CP))
         g.wait_ge(S.v, vp)
         if flat:
-            to_roots(u8(oq), u8(oq), S["qc" + n])
+            to_roots(t, u8(oq), u8(oq), S["qc" + n])
             g.wait_ge(S.s, own_s)
-            to_roots(op, op, S["qs" + n])
+            to_roots(t, op, op, S["qs" + n], "ls" if root or last else "lw")
         elif root:
             to_peers(u8(oq), u8(oq), S["qc" + n])
             g.wait_ge(S.s, own_s)
@@ -406,53 +411,73 @@ def rank_program(g, core, T, topo):
             to_mate(u8(T["xq" + n][:, FED:HEAD]), u8(oq), S["yc" + n])
             g.wait_ge(S.s, own_s)
             to_mate(T["xp" + n][:, FED:HEAD], op, S["ys" + n])
+        if t == 1:
+            V(lambda: vec.memset(T.yo[:], 0.0), after=0)
+            for_roots()
+            if root:
+                g.scalar.wait_ge(S.v, zeros("m", 1))
+                send_number(t)
         if not root:
-            yo = T["yo" + n][:, 0:1]
-            g.wait_ge(S.v, V(lambda: vec.tensor_scalar(yo, ct, -1.0, bnum, A.mult, A.add), after=0))
-            to_mate(T["yn" + n][:, 0:1], yo, S["yn" + n])
-            if t < R:
+            if not last:
+                if not flat:
+                    send_number(t, "lw" if t < 3 else "ls")
+                if t < 3:
+                    g.sync.wait_ge(S.lw, cnt["lw"])
+                    g.sync.dma_start(T.wb[:], T.w[:]).then_inc(S.ld_w, 16)
+                    V(lambda: vec.memset(ql[:], 0.0), after=0)
+                if t > 1:
+                    V(lambda: vec.tensor_scalar(cf(MINE), fg, float(ab), None, A.is_equal), after=0)
+                if t == 3:
+                    V(lambda: vec.tensor_scalar(cf(LAST), fg, 3.0, None, A.is_equal), after=0)
+                    V(lambda: vec.tensor_scalar(cf(FIRST), fg, 2.0, None, A.is_equal), after=0)
+                    V(lambda: vec.memset(T.res[:], 0.0), after=0)
                 for name, u in shadow[t]:
                     zd = zeros(name, u)
                 g.scalar.wait_ge(S.v, zd)
-                for c in cols:
-                    quant_x(source[t + 1], *c)
             if t < 3:
+                quant_x(source[t + 1], 0, 512)
+                quant_x(source[t + 1], 512, 512)
+            else:
                 vec.wait_ge(S.ld_w, 16)
-                wdone[0] = V(lambda: vec.quantize_mx(T.wq[:, 0:128 * O], T.wp[:, 0:128 * O], T.wb[:, 0:512 * O]), after=0)
-            for f in later:
-                f()
-            later = []
+                wdone[0] = V(lambda: vec.quantize_mx(T.wq[:, 0:128 * O], T.wp[:, 0:128 * O], T.wb[:, 0:512 * O]))
+            if t == 3:
+                c2, c1 = tmp(), tmp()
+                numbers(2, c2)
+                numbers(1, c1)
+                V(lambda: vec.tensor_tensor(lo(ql, 4 * rank, 2), c1, c2, A.add))
             if t > 1:
                 g.sync.wait_ge(S.v, cnt["v"])
                 store(t - 1, (S.v, picked[t - 1][0]), (S.s, picked[t - 1][1]))
-                products(t - 1)
-            if t == R:
-                g.sync.wait_ge(S.v, resolve())
-                rows(T.res, ab)
+            if t > 2:
+                for u in range(1, t):
+                    products(u)
+            if last:
+                g.sync.wait_ge(S.s, cnt["s"])
+                for o in range(O):
+                    ystore(g.sync, 64 * o, 64 * o + 48)
             vec.wait_ge(S.v, cnt["v"])
             cnt["vw"] = cnt["v"]
         dq, dp = T["dq" + n], T["dp" + n]
-        es = last_es if t == R else EM
         if root:
-            if t == R:
-                numbers(t, e, None, ct)
             a = 16 * t
-            rm, rl = T.rm[:, a + 1:a + 1 + nslot], T.rm[:, a + nslot:a + nslot + 1]
-            ns = T.ns[:, t:t + 1]
+            run = 1 if last else 0
+            p0, p1 = 32 * run, 32 * run + 32
+            rm, rl = T.rm[p0:p1, a + 1:a + 1 + nslot], T.rm[p0:p1, a + nslot:a + nslot + 1]
+            ns = lo(T.ns, t, run)
             inc = FLAT_INC if flat else PEER_INC
             vec.wait_ge(S["qm" + n], inc)
-            if flat:
+            if flat and not last:
                 vec.wait_ge(S.s, scp)
-            v = V(lambda: vec.tensor_tensor_scan(rm, qm[:, 0:4 * nslot:4], qm[:, 0:4 * nslot:4], FAR, A.min, A.min), after=vo)
+            marks = qm[p0:p1, 0:4 * nslot:4]
+            v = V(lambda: vec.tensor_tensor_scan(rm, marks, marks, FAR, A.min, A.min), after=None if t == 1 else vo)
             g.scalar.wait_ge(S.v, v)
-            sns = AC(lambda: act(T.sh[:, a:a + nslot + 1], T.rm[:, a:a + nslot + 1], ACT.Sign, bias=rl, scale=-1.0, accum_out=ns))
+            sns = AC(lambda: act(T.sh[p0:p1, a:a + nslot + 1], T.rm[p0:p1, a:a + nslot + 1], ACT.Sign, bias=rl, scale=-1.0,
+                                 accum_out=ns))
             vec.wait_ge(S.s, sns)
             lst = T["cm" + n]
             off2 = lst[:, 8:9]
-            vo = spread(lambda a, b: vec.tensor_scalar(lst[a:b, 0:10], T.kt[0:32, 0:10], lo(T.ns, t), lo(T.cf, B112),
+            vo = spread(lambda a, b: vec.tensor_scalar(lst[a:b, 0:10], T.kt[p0:p1, 0:10], ns, lo(T.cf, B112, run),
                                                        A.mult, A.add), 0)
-            if t > 1:
-                products(t - 1)
             vec.wait_ge(S["qc" + n], inc)
             g.scalar.wait_ge(S["qs" + n], inc)
             wid = ZERO + 16 * nslot
@@ -461,38 +486,43 @@ def rank_program(g, core, T, topo):
             sp_ = AC(lambda: act(dp[:, 128:144], mp[:, 0:wid].indirect(off2), CP), after=sns)
             picked[t] = (vp, sp_)
             g.wait_ge(S.v, vp)
-            to_mate(u8(dq[:, 128:144]), u8(dq[:, 128:144]), S["dc" + n], es)
+            to_mate(u8(dq[:, 128:144]), u8(dq[:, 128:144]), S["dc" + n])
             g.wait_ge(S.s, sp_)
             to_mate(dp[:, 128:144], dp[:, 128:144], S["ds" + n])
-            if t < R:
-                windows(t + 1, mq[:, 0:wid], mp[:, 0:wid], lst)
-                later.append(lambda t=t, e=e, ns=ns, ct=ct: (numbers(t, e, ns, ct), which_slot(t, ns)))
+            if not last:
+                windows(t + 1, mq[:, 0:wid], mp[:, 0:wid], lst, (S["qs" + n], inc))
+                if t + 1 == R:
+                    numbers(t, lo(ql, 4 * rank, 3))
             else:
+                v = resolve()
+                g.wait_ge(S.v, v)
+                to_mate(T.resl[:, 0:1], T.res[:, 0:1], S.rs)
                 store(t, (S.v, vp), (S.s, sp_))
+                products(R - 1)
                 products(R)
-                which_slot(t, ns)
-        else:
-            if t < R:
-                vec.wait_ge(S["dc" + n], len(es))
-                g.scalar.wait_ge(S["ds" + n], MATE_INC)
-                windows(t + 1, dq[:, 0:144], dp[:, 0:144], T.cl)
-            else:
-                g.tensor.wait_ge(S["dc" + n], len(es))
-                g.tensor.wait_ge(S["ds" + n], MATE_INC)
-            store(t, (S["dc" + n], len(es)), (S["ds" + n], MATE_INC))
-            if t == R:
-                products(R)
-        if t == R:
-            g.scalar.wait_ge(S.s, cnt["s"])
-            g.scalar.dma_start(T.y[:], T.ysb[:]).then_inc(S.sty, 16)
-            v = resolve() if root else 0
-            g.sync.wait_ge(S.rs, MATE_INC)
-            rows(T.resl, 1 - ab)
-            if root:
                 g.sync.wait_ge(S.v, v)
-                rows(T.res, ab)
+                store_nb(T.res)
+                g.scalar.wait_ge(S.s, cnt["s"])
+                ystore(g.scalar, 0, 64 * O)
+        else:
+            if not last:
+                vec.wait_ge(S["dc" + n], MATE_INC)
+                g.scalar.wait_ge(S["ds" + n], MATE_INC)
+                windows(t + 1, dq[:, 0:144], dp[:, 0:144], T.cl, (S["ds" + n], MATE_INC))
+            else:
+                g.tensor.wait_ge(S["dc" + n], MATE_INC)
+                g.tensor.wait_ge(S["ds" + n], MATE_INC)
+            store(t, (S["dc" + n], MATE_INC), (S["ds" + n], MATE_INC))
+            if last:
+                v = products(R)
+                g.sync.wait_ge(S.rs, MATE_INC)
+                store_nb(T.resl)
+                g.scalar.wait_ge(S.s, cnt["s"])
+                ystore(g.scalar, 48, 64)
+                g.sync.wait_ge(S.v, v)
+                ystore(g.sync, 112, 128)
     g.sync.wait_ge(S.st, cnt["st"])
-    g.scalar.wait_ge(S.sty, 16)
+    g.scalar.wait_ge(S.sty, cnt["sty"])
     g.wait_ge(S.ls, cnt["ls"])
     g.wait_ge(S.v, cnt["v"])
     g.wait_ge(S.s, cnt["s"])

from concourse.bass import DstId, RemoteDMATransfer
from concourse.mybir import dt, AluOpType, AxisListType, ActivationFunctionType

R, P, O, N = 4, 1024, 2, 8
HEAD = 144
FED = HEAD - 16
ZERO = FED
FLAT = (1, R)
PIECES = [(0, 512), (512, 256), (768, 128), (896, 128)]
F8 = "float8_e4m3fn_x4"
SCRATCH = {
    "xb": ("sbuf", [128, 4 * P], "bfloat16"),
    "wb": ("sbuf", [128, 512 * O], "bfloat16"),
    "sd": ("sbuf", [128, 576], "bfloat16"),
    "wq": ("sbuf", [128, 128 * O], F8), "wp": ("sbuf", [128, 128 * O], "uint8"),
    "ip": ("sbuf", [128, 8], "int32"),
    "q8": ("sbuf", [128, 8], "float32"),
    "kt": ("sbuf", [128, 16], "float32"),
    "rm": ("sbuf", [128, 16 * (R + 1)], "float32"),
    "j4": ("sbuf", [128, 256], "float32"),
    "ja": ("sbuf", [128, 256], "float32"),
    "c8": ("sbuf", [128, 8], "float32"),
    "k8": ("sbuf", [128, 8], "float32"),
    "kv": ("sbuf", [128, 8], "float32"),
    "cf": ("sbuf", [128, 16], "float32"),
    "cl": ("sbuf", [128, 8], "uint16"),
    "sg": ("sbuf", [128, 128 * (R + 1)], "bfloat16"),
    "sh": ("sbuf", [128, 16 * (R + 1)], "bfloat16"),
    "ct": ("sbuf", [128, 8], "float32"),
    "yo": ("sbuf", [128, 4 * R], "float32"),
    "ns": ("sbuf", [128, 8], "float32"),
    "ee": ("sbuf", [128, 8], "float32"),
    "tmp": ("sbuf", [128, 64], "float32"),
    "ofs": ("sbuf", [128, 32], "uint16"),
    "res": ("sbuf", [128, 4], "float32"),
    "resl": ("sbuf", [128, 4], "float32"),
    "ysb": ("sbuf", [128, 64 * O], "float32"),
    "ps": ("psum", [128, 1024], "float32"),
}
for _t in range(R + 1):
    if _t in (0, 2, 3):
        SCRATCH["xq%d" % _t] = ("sbuf", [128, HEAD + P], F8)
        SCRATCH["xp%d" % _t] = ("sbuf", [128, HEAD + P], "uint8")
    SCRATCH["dq%d" % _t] = ("sbuf", [128, ZERO + 16], F8)
    SCRATCH["dp%d" % _t] = ("sbuf", [128, ZERO + 16], "uint8")
    SCRATCH["mk%d" % _t] = ("sbuf", [128, 256], "float32")
    if _t:
        _m = N if _t in FLAT else N // 2
        SCRATCH["rn%d" % _t] = ("sbuf", [128, 128], "float32")
        SCRATCH["cm%d" % _t] = ("sbuf", [128, 16], "uint16")
        SCRATCH["mq%d" % _t] = ("sbuf", [128, ZERO + 16 * _m], F8)
        SCRATCH["mp%d" % _t] = ("sbuf", [128, ZERO + 16 * _m], "uint8")
        SCRATCH["qm%d" % _t] = ("sbuf", [128, 4 * _m], "float32")
    if _t > 1:
        SCRATCH["wc%d" % _t] = ("sbuf", [128, 256], F8)
        SCRATCH["ws%d" % _t] = ("sbuf", [128, 256], "uint8")
    if 0 < _t < R:
        SCRATCH["yn%d" % _t] = ("sbuf", [128, 4], "float32")
    if 1 < _t < R:
        SCRATCH["pq%d" % _t] = ("sbuf", [128, 16], F8)
        SCRATCH["pp%d" % _t] = ("sbuf", [128, 16], "uint8")
        SCRATCH["ym%d" % _t] = ("sbuf", [128, 4], "float32")
for _k in range(6):
    SCRATCH["py%d" % _k] = ("psum", [128, 512], "float32")
SEMAPHORES = ["v", "s", "t", "ty", "iot", "iou", "ls", "lw", "ld_s", "ld_w", "st", "sty", "rs", "wc", "ws"]
SEMAPHORES += ["ld%d" % q for q in range(len(PIECES))]
SEMAPHORES += [n + "%d" % t for t in range(1, R + 1) for n in ("ym", "yn", "yc", "ys", "qm", "qc", "qs", "dc", "ds")]

FAR = 1e29


def rank_program(g, core, T, topo):
    rank = T.rank_of(core)
    if rank is None:
        return
    A = AluOpType
    X = AxisListType.X
    ACT = ActivationFunctionType
    CP, ID = ACT.Copy, ACT.Identity
    S = T.sem
    chips, ranks_of = [], {}
    for c in T.cores:
        if topo.chip(c) not in ranks_of:
            chips.append(topo.chip(c))
            ranks_of[topo.chip(c)] = []
        ranks_of[topo.chip(c)].append(c)
    me = chips.index(topo.chip(core))
    ab = ranks_of[chips[me]].index(core)
    mate = ranks_of[chips[me]][1 - ab]
    nch = len(chips)
    others = [chips[(me + k) % nch] for k in range(1, nch)]
    peers = [ranks_of[h][ab] for h in others]

    cnt = {"v": 0, "vw": 0, "s": 0, "sw": 0, "ty": 0, "ls": 0, "lw": 0, "st": 0, "sty": 0}

    def V(call, after=None):
        need = cnt["v"] if after is None else after
        if cnt["vw"] < need:
            g.vector.wait_ge(S.v, need)
            cnt["vw"] = need
        call().then_inc(S.v, 1)
        cnt["v"] += 1
        return cnt["v"]

    def AC(call, after=0):
        if cnt["sw"] < after:
            g.scalar.wait_ge(S.s, after)
            cnt["sw"] = after
        call().then_inc(S.s, 1)
        cnt["s"] += 1
        return cnt["s"]

    def bits(es):
        return sum(1 << e for e in es)

    def dst(c):
        a = topo.addr(c)
        return DstId(rid=a[0], pnc=a[1])

    ES = topo.engines(core, peers[0])[:8]
    EM = topo.engines(core, mate)[:16]
    EO = [e for e in EM if e not in ES][:8]
    MATE_INC = len(EM)
    PEER_INC = len(ES) * len(peers)
    FLAT_INC = 2 * PEER_INC + len(EO)

    def to_mate(out, in_, sem, left="ls"):
        rid, pid = topo.addr(mate)[:2]
        g.remote_dma(out, in_, sem, S[left], pid, rid, bits(EM))
        cnt[left] += len(EM)

    def fused(parts, left="ls"):
        g.remote_dma_fused([RemoteDMATransfer(dst_ids=[dst(c) for c in cs], dma_engine_mask=bits(e), remote_sem=sem,
                                              srcs=[in_], dsts=[out] * len(cs))
                            for cs, e, out, in_, sem in parts], local_sem=S[left])
        cnt[left] += sum(len(p[1]) for p in parts)

    def to_peers(out, in_, sem):
        fused([(peers, ES, out, in_, sem)])

    def to_roots(t, out, in_, sem, left="ls"):
        who = (t - 1) % 2
        parts = [([ranks_of[h][who] for h in others], ES, out, in_, sem)]
        fused(parts if ab == who else parts + [([mate], EO, out, in_, sem)], left)

    def u8(ap):
        return ap.bitcast(dt.uint8)

    def u32(ap):
        return ap.bitcast(dt.uint32)

    tcol = [0]

    def tmp(n=1):
        a = tcol[0]
        tcol[0] += n
        return T.tmp[0:32, a:a + n]

    vec = g.vector
    act = g.scalar.activation
    g.scalar.dma_start(T.sd[:, 512:576], T.seed[:]).then_inc(S.ld_s, 16)
    for k, (a, n) in enumerate(PIECES):
        g.scalar.dma_start(T.xb[:, 4 * a:4 * (a + n)], T.x[:, 4 * a:4 * (a + n)]).then_inc(S["ld%d" % k], 16)

    g.iota(T.ip[:, 0:1], [[0, 1]], ZERO, 1).then_inc(S.iot, 1)
    g.iota(T.q8[:], [[1, 4], [0, 2]], 0, 0, allow_small_or_imprecise_dtypes=True).then_inc(S.iot, 1)
    g.iota(T.j4[:], [[1, 4], [0, 64]], 0, 0, allow_small_or_imprecise_dtypes=True).then_inc(S.iou, 1)
    g.iota(T.c8[:], [[-1, N]], -1, 0, allow_small_or_imprecise_dtypes=True).then_inc(S.iou, 1)
    g.iota(T.k8[:], [[P, N]], -HEAD, 0, allow_small_or_imprecise_dtypes=True).then_inc(S.iou, 1)

    def cf(k):
        return T.cf[:, k:k + 1]

    def lo(buf, k, run=0):
        return buf[32 * run:32 * run + 32, k:k + 1]

    def zeros(name, t):
        if name == "w":
            return V(lambda: vec.quantize_mx(T["wc%d" % t][:, 128:256], T["ws%d" % t][:, 128:256], T.sd[:, 0:512]), after=0)
        return V(lambda: vec.quantize_mx(T["%sq%d" % (name, t)][:, 0:ZERO], T["%sp%d" % (name, t)][:, 0:ZERO], T.sd[:, 0:512]), after=0)

    def spread(call, after):
        for k in range(4):
            v = V(lambda: call(32 * k, 32 * k + 32), after=after)
        return v

    ql = T["qm%d" % R]
    V(lambda: vec.memset(T.sd[:, 0:512], 0.0))
    vec.wait_ge(S.iot, 2)
    V(lambda: vec.tensor_scalar(T.ip[:, 1:2], T.ip[:, 0:1], ZERO + 15, None, A.bitwise_and), after=0)
    V(lambda: vec.tensor_scalar(T.ip[:, 2:3], T.ip[:, 0:1], 2, 3, A.logical_shift_right, A.bitwise_and), after=0)
    V(lambda: vec.tensor_scalar(T.ip[:, 3:4], T.ip[:, 0:1], 3, None, A.bitwise_and), after=0)
    V(lambda: vec.tensor_scalar(T.ip[:, 4:5], T.ip[:, 0:1], 1, 7, A.logical_shift_right, A.bitwise_and), after=0)
    V(lambda: vec.tensor_scalar(T.ip[:, 5:6], T.ip[:, 0:1], 4, 7, A.logical_shift_right, A.bitwise_and), after=0)
    vc = V(lambda: vec.tensor_copy(T.cf[:, 0:5], T.ip[:, 1:6]))
    b128, fq, fr, fh, fg = cf(0), cf(1), cf(2), cf(3), cf(4)
    B128, BASE, BNUM, MINE, LAST, FIRST, B112 = 0, 6, 7, 8, 9, 10, 13
    base, bnum = cf(BASE), cf(BNUM)
    V(lambda: vec.tensor_scalar(T.cl[:], T.q8[:], fq, b128, A.is_equal, A.mult))
    vec.wait_ge(S.ld_s, 16)
    d0_done = V(lambda: vec.quantize_mx(T.dq0[:, 0:144], T.dp0[:, 0:144], T.sd[:, 0:576]), after=0)
    V(lambda: vec.tensor_copy(u32(T.xq0[:, 16:HEAD]), u32(T.dq0[:, 0:144]).indirect(T.cl[:, 0:8])))

    def for_roots():
        V(lambda: vec.memset(T.rm[:], FAR), after=0)
        V(lambda: vec.memset(T.kt[:, 8:16], -16.0), after=0)
        V(lambda: vec.tensor_scalar(T.kt[:, 0:8], T.q8[:], fq, -16.0, A.is_equal, A.mult), after=0)
        zeros("w", 2)

    def windows(t, q0, p0, lst, scales):
        wc, ws = T["wc%d" % t], T["ws%d" % t]
        vec.tensor_copy(u32(wc[:, 96:128]), u32(q0).indirect(lst[:, 6:8])).then_inc(S.wc, 1)
        vec.wait_ge(*scales)
        vec.tensor_copy(ws[:, 96:128], p0.indirect(lst[:, 6:8])).then_inc(S.wc, 1)
        vec.tensor_copy(u32(wc[:, 0:96]), u32(q0).indirect(lst[:, 0:6])).then_inc(S.wc, 1)
        act(ws[:, 0:96], p0.indirect(lst[:, 0:6]), CP).then_inc(S.ws, 1)

    g.scalar.wait_ge(S.v, vc)
    sb = AC(lambda: act(base, fh, ID, bias=float(HEAD), scale=128.0))
    AC(lambda: act(bnum, fh, ID, bias=float(P * rank), scale=128.0))
    AC(lambda: act(cf(B112), b128, ID, bias=-16.0, scale=1.0))
    g.scalar.wait_ge(S.iou, 3)
    sj = AC(lambda: act(T.ja[:], T.j4[:], ACT.Abs, bias=fr, scale=-1.0))
    g.scalar.wait_ge(S.v, d0_done)
    s1_done = AC(lambda: act(T.xp0[:, 16:HEAD], T.dp0[:, 0:144].indirect(T.cl[:, 0:8]), CP))
    AC(lambda: act(T.kv[:], T.k8[:], ID, bias=base, scale=1.0), after=sb)
    consts = AC(lambda: act(T.mk0[:], T.ja[:], ID, bias=-FAR, scale=2 * FAR), after=sj)

    def quant_x(k, a, n):
        return V(lambda: vec.quantize_mx(T["xq%d" % k][:, HEAD + a:HEAD + a + n], T["xp%d" % k][:, HEAD + a:HEAD + a + n],
                                         T.xb[:, 4 * a:4 * (a + n)]), after=0)

    xdone = []
    for k, (a, n) in enumerate(PIECES):
        vec.wait_ge(S["ld%d" % k], 16)
        xdone += [quant_x(0, a, n)] * (n // 128)
    vec.wait_ge(S.s, consts)
    source = {1: 0, 2: 0, 3: 3, 4: 3} if ab == 0 else {1: 0, 2: 2, 3: 2, 4: 2}

    def score(t):
        if t == 1:
            order = [(q, h) for q in range(4) for h in range(2)]
            wc, ws = T.xq0, T.xp0
            g.tensor.wait_ge(S.s, s1_done)
        else:
            order = [(3, 0), (3, 1), (2, 0), (1, 0), (0, 0), (2, 1), (1, 1), (0, 1)]
            wc, ws = T["wc%d" % t], T["ws%d" % t]
            g.tensor.wait_ge(S.wc, 3 * t - 4)
        seen, rest = [0, 0], t == 1
        for q, h in order:
            if q < 3 and not rest:
                g.tensor.wait_ge(S.wc, 3 * t - 3)
                g.tensor.wait_ge(S.ws, t - 1)
                rest = True
            if t == 1:
                g.tensor.wait_ge(S.v, xdone[2 * q + h])
            a, c = HEAD + 256 * q + 128 * h, 32 * q + (16 if t == 1 else 0)
            seen[h] += 1
            i = g.tensor.matmul_mx(T.ps[:, 512 * h:512 * h + 128], wc[:, c:c + 128], ws[:, c:c + 128],
                                   T.xq0[:, a:a + 128], T.xp0[:, a:a + 128], seen[h] == 1, seen[h] == 4)
            if seen[h] == 4:
                i.then_inc(S.t, 1)

    ydone, wdone, picked = {}, [0], {}

    def ystore(queue, a, b):
        queue.dma_start(T.y[:, a:b], T.ysb[:, a:b]).then_inc(S.sty, 16)
        cnt["sty"] += 16

    def products(t):
        k = 2 * ((t - 1) % 3)
        if t == 1:
            g.tensor.wait_ge(S.v, wdone[0])
        if t == 4:
            g.tensor.wait_ge(S.s, ydone[1])
        if t in picked:
            g.tensor.wait_ge(S.v, picked[t][0])
            g.tensor.wait_ge(S.s, picked[t][1])
        for o in range(O):
            g.tensor.matmul_mx(T["py%d" % (k + o)][:, 0:128], T.wq[:, 128 * o:128 * o + 128], T.wp[:, 128 * o:128 * o + 128],
                               T["dq%d" % t][:, 16:144], T["dp%d" % t][:, 16:144], True, True).then_inc(S.ty, 1)
            cnt["ty"] += 1
        both = t == R and ab == 0
        v = 0
        for o in range(O):
            out, in_ = T.ysb[:, 64 * o + 16 * (t - 1):64 * o + 16 * t], T["py%d" % (k + o)][:, 112:128]
            if both and o == 1:
                vec.wait_ge(S.ty, cnt["ty"])
                v = V(lambda: vec.tensor_copy(out, in_), after=0)
            else:
                g.scalar.wait_ge(S.ty, cnt["ty"] - O + 1 + o)
                ydone[t] = AC(lambda: act(out, in_, CP))
        return v

    def store(t, codes, scales):
        dq, dp = T["dq%d" % t], T["dp%d" % t]
        g.sync.wait_ge(*codes)
        g.sync.dma_start(T.oc[:, 64 * (t - 1):64 * t], u8(dq[:, 128:144])).then_inc(S.st, 16)
        g.sync.wait_ge(*scales)
        for k in range(4):
            g.sync.dma_start(T.osc[4 * k:4 * k + 4, 16 * (t - 1):16 * t], dp[32 * k:32 * k + 4, 128:144]).then_inc(S.st, 16)
        cnt["st"] += 80

    def store_nb(buf):
        g.sync.dma_start(T.nb[:], buf[64:128, 0:1]).then_inc(S.st, 16)
        cnt["st"] += 16

    def send_number(t, left="ls"):
        v = V(lambda: vec.tensor_scalar(lo(T.yo, 4 * t), lo(T.ct, t), -1.0, lo(T.cf, BNUM), A.mult, A.add),
              after=None if t == 1 else 0)
        if t == 2:
            v = V(lambda: vec.tensor_copy(lo(T.yo, 4 * t, 1), lo(T.ns, 1)), after=0)
        g.wait_ge(S.v, v)
        to_mate(T["yn%d" % t][:, 0:1], T.yo[:, 4 * t:4 * t + 1], S["yn%d" % t], left)

    def numbers(t, out):
        ns, ct, yn = lo(T.ns, t), lo(T.ct, t), lo(T["yn%d" % t], 0)
        own, won, a, b = tmp(), tmp(), tmp(), tmp()
        V(lambda: vec.tensor_scalar(own, ct, -1.0, lo(T.cf, BNUM), A.mult, A.add), after=0)
        vec.wait_ge(S["yn%d" % t], MATE_INC)
        if t in FLAT:
            V(lambda: vec.tensor_scalar(won, lo(T.yn2, 0, 1), lo(T.cf, FIRST, 1), None, A.mult), after=0)
            v = V(lambda: vec.tensor_scalar(a, won, -float(rank + 1), own, A.is_equal, A.mult))
            V(lambda: vec.tensor_scalar(b, won, -float(T.rank_of(mate) + 1), yn, A.is_equal, A.mult), after=v - 1)
            return V(lambda: vec.tensor_tensor(out, a, b, A.add))
        V(lambda: vec.tensor_scalar(won, ns, -float(me + 1), lo(T.cf, MINE), A.is_equal, A.mult), after=0)
        V(lambda: vec.tensor_tensor(a, yn, own, A.subtract), after=cnt["v"] - 1)
        V(lambda: vec.tensor_scalar(b, lo(T.ee, t), 0.0, a, A.is_equal, A.mult))
        return V(lambda: vec.tensor_scalar(out, b, own, won, A.add, A.mult))

    def resolve():
        val, oh = tmp(N), tmp(N)
        V(lambda: vec.tensor_tensor(val, T.kv[0:32, :], ql[0:32, 0:4 * N:4], A.subtract), after=0)
        V(lambda: vec.tensor_scalar(oh, T.c8[32:64, :], lo(T.ns, R, 1), lo(T.cf, LAST, 1), A.is_equal, A.mult), after=0)
        V(lambda: vec.tensor_tensor(ql[96:128, 1:4 * N:4], oh, val, A.mult))
        return V(lambda: vec.tensor_reduce(T.res[64:128, 0:1], ql[64:128, :], X, A.add))

    shadow = {1: [("d", 1), ("w", 3), ("m", 2)], 3: [("d", 2), ("d", 3), ("d", 4), ("w", 4)],
              2: [("d", 1), ("d", 2), ("d", 3), ("d", 4), ("w", 3), ("w", 4), ("m", 3)]}
    for t in range(1, R + 1):
        root, flat, last = (t - 1) % 2 == ab, t in FLAT, t == R
        merge = root and not flat
        n = "%d" % t
        mk, qm, rn = T["mk" + n], T["qm" + n], T["rn" + n]
        slot = rank if flat else me
        nslot = N if flat else nch
        mq, mp = T["mq" + n], T["mp" + n]
        mine = qm[:, 4 * slot:4 * slot + 1]
        score(t)
        for h in range(2):
            vec.wait_ge(S.t, 2 * t - 1 + h)
            V(lambda: vec.tensor_tensor(mk[:, 128 * h:128 * h + 128], T["mk%d" % (t - 1)][:, 128 * h:128 * h + 128],
                                        T.ps[:, 512 * h:512 * h + 128], A.max), after=0)
        vr = V(lambda: vec.tensor_tensor_scan(rn[:], mk[:, 0:128], mk[:, 128:256], FAR, A.min, A.min))
        low = rn[:, 127:128]
        g.scalar.wait_ge(S.v, vr)
        ct = lo(qm, 4 * slot) if last else lo(T.ct, t)
        sct = AC(lambda: act(T.sg[0:32, 128 * t:128 * t + 128], rn[0:32, :], ACT.Sign, bias=lo(rn, 127), scale=-1.0,
                             accum_out=ct))
        off = T.ofs[:, 4 * t:4 * t + 1]
        sq, sp = T["xq%d" % source[t]], T["xp%d" % source[t]]
        if merge:
            ym = T["ym" + n][:, 0:1]
            vec.wait_ge(S["ym" + n], MATE_INC)
            vm = V(lambda: vec.tensor_tensor(mine, ym, low, A.min), after=vr)
            ve = V(lambda: vec.tensor_scalar(T.ee[:, t:t + 1], ym, low, base, A.is_ge if ab == 0 else A.is_gt, A.mult),
                   after=vr)
            g.wait_ge(S.v, vm)
            to_peers(mine, mine, S["qm" + n])
            vec.wait_ge(S.s, sct)
            vo = spread(lambda a, b: vec.tensor_scalar(T.ofs[a:b, 4 * t:4 * t + 1], lo(T.ee, t), ct, lo(T.cf, B128),
                                                       A.subtract, A.max), ve)
            vec.wait_ge(S["yc" + n], MATE_INC)
        else:
            if last:
                vm = V(lambda: vec.tensor_copy(lo(qm, 4 * slot, 1), lo(rn, 127)), after=vr)
                g.wait_ge(S.v, vm)
                g.wait_ge(S.s, sct)
                to_roots(t, mine, mine, S["qm" + n])
            else:
                g.wait_ge(S.v, vr)
                if flat:
                    to_roots(t, mine, low, S["qm" + n])
                    if root:
                        scp = AC(lambda: act(mine, low, CP))
                else:
                    to_mate(T["ym" + n][:, 0:1], low, S["ym" + n])
            vec.wait_ge(S.s, sct)
            vo = spread(lambda a, b: vec.tensor_scalar(T.ofs[a:b, 4 * t:4 * t + 1], ct, -1.0, lo(T.cf, BASE),
                                                       A.mult, A.add), vr)
        if flat or root:
            a = ZERO + 16 * slot
            oq, op = mq[:, a:a + 16], mp[:, a:a + 16]
        else:
            oq, op = T["pq" + n][:, 0:16], T["pp" + n][:, 0:16]
        vp = V(lambda: vec.tensor_copy(u32(oq), u32(sq[:, 0:HEAD + P]).indirect(off)), after=vo)
        g.scalar.wait_ge(S.v, vo)
        if merge:
            g.scalar.wait_ge(S["ys" + n], MATE_INC)
        own_s = AC(lambda: act(op, sp[:, 0:HEAD + P].indirect(off), CP))
        g.wait_ge(S.v, vp)
        if flat:
            to_roots(t, u8(oq), u8(oq), S["qc" + n])
            g.wait_ge(S.s, own_s)
            to_roots(t, op, op, S["qs" + n], "ls" if root or last else "lw")
        elif root:
            to_peers(u8(oq), u8(oq), S["qc" + n])
            g.wait_ge(S.s, own_s)
            to_peers(op, op, S["qs" + n])
        else:
            to_mate(u8(T["xq" + n][:, FED:HEAD]), u8(oq), S["yc" + n])
            g.wait_ge(S.s, own_s)
            to_mate(T["xp" + n][:, FED:HEAD], op, S["ys" + n])
        if t == 1:
            V(lambda: vec.memset(T.yo[:], 0.0), after=0)
            for_roots()
            if root:
                g.scalar.wait_ge(S.v, zeros("m", 1))
                send_number(t)
        if not root:
            if not last:
                if not flat:
                    send_number(t, "lw" if t < 3 else "ls")
                if t < 3:
                    g.sync.wait_ge(S.lw, cnt["lw"])
                    g.sync.dma_start(T.wb[:], T.w[:]).then_inc(S.ld_w, 16)
                    V(lambda: vec.memset(ql[:], 0.0), after=0)
                if t > 1:
                    V(lambda: vec.tensor_scalar(cf(MINE), fg, float(ab), None, A.is_equal), after=0)
                if t == 3:
                    V(lambda: vec.tensor_scalar(cf(LAST), fg, 3.0, None, A.is_equal), after=0)
                    V(lambda: vec.tensor_scalar(cf(FIRST), fg, 2.0, None, A.is_equal), after=0)
                    V(lambda: vec.memset(T.res[:], 0.0), after=0)
                for name, u in shadow[t]:
                    zd = zeros(name, u)
                g.scalar.wait_ge(S.v, zd)
            if t < 3:
                quant_x(source[t + 1], 0, 512)
                quant_x(source[t + 1], 512, 512)
            else:
                vec.wait_ge(S.ld_w, 16)
                wdone[0] = V(lambda: vec.quantize_mx(T.wq[:, 0:128 * O], T.wp[:, 0:128 * O], T.wb[:, 0:512 * O]))
            if t == 3:
                c2, c1 = tmp(), tmp()
                numbers(2, c2)
                numbers(1, c1)
                V(lambda: vec.tensor_tensor(lo(ql, 4 * rank, 2), c1, c2, A.add))
            if t > 1:
                g.sync.wait_ge(S.v, cnt["v"])
                store(t - 1, (S.v, picked[t - 1][0]), (S.s, picked[t - 1][1]))
            if t > 2:
                for u in range(1, t):
                    products(u)
            if last:
                g.sync.wait_ge(S.s, cnt["s"])
                for o in range(O):
                    ystore(g.sync, 64 * o, 64 * o + 48)
            vec.wait_ge(S.v, cnt["v"])
            cnt["vw"] = cnt["v"]
        dq, dp = T["dq" + n], T["dp" + n]
        if root:
            a = 16 * t
            run = 1 if last else 0
            p0, p1 = 32 * run, 32 * run + 32
            rm, rl = T.rm[p0:p1, a + 1:a + 1 + nslot], T.rm[p0:p1, a + nslot:a + nslot + 1]
            ns = lo(T.ns, t, run)
            inc = FLAT_INC if flat else PEER_INC
            vec.wait_ge(S["qm" + n], inc)
            if flat and not last:
                vec.wait_ge(S.s, scp)
            marks = qm[p0:p1, 0:4 * nslot:4]
            v = V(lambda: vec.tensor_tensor_scan(rm, marks, marks, FAR, A.min, A.min), after=None if t == 1 else vo)
            g.scalar.wait_ge(S.v, v)
            sns = AC(lambda: act(T.sh[p0:p1, a:a + nslot + 1], T.rm[p0:p1, a:a + nslot + 1], ACT.Sign, bias=rl, scale=-1.0,
                                 accum_out=ns))
            vec.wait_ge(S.s, sns)
            lst = T["cm" + n]
            off2 = lst[:, 8:9]
            vo = spread(lambda a, b: vec.tensor_scalar(lst[a:b, 0:10], T.kt[p0:p1, 0:10], ns, lo(T.cf, B112, run),
                                                       A.mult, A.add), 0)
            vec.wait_ge(S["qc" + n], inc)
            g.scalar.wait_ge(S["qs" + n], inc)
            wid = ZERO + 16 * nslot
            vp = V(lambda: vec.tensor_copy(u32(dq[:, 128:144]), u32(mq[:, 0:wid]).indirect(off2)), after=vo)
            g.scalar.wait_ge(S.v, vo)
            sp_ = AC(lambda: act(dp[:, 128:144], mp[:, 0:wid].indirect(off2), CP), after=sns)
            picked[t] = (vp, sp_)
            g.wait_ge(S.v, vp)
            to_mate(u8(dq[:, 128:144]), u8(dq[:, 128:144]), S["dc" + n])
            g.wait_ge(S.s, sp_)
            to_mate(dp[:, 128:144], dp[:, 128:144], S["ds" + n])
            if not last:
                windows(t + 1, mq[:, 0:wid], mp[:, 0:wid], lst, (S["qs" + n], inc))
                if t + 1 == R:
                    numbers(t, lo(ql, 4 * rank, 3))
            else:
                v = resolve()
                g.wait_ge(S.v, v)
                to_mate(T.resl[:, 0:1], T.res[:, 0:1], S.rs)
                store(t, (S.v, vp), (S.s, sp_))
                products(R - 1)
                products(R)
                g.sync.wait_ge(S.v, v)
                store_nb(T.res)
                g.scalar.wait_ge(S.s, cnt["s"])
                ystore(g.scalar, 0, 64 * O)
        else:
            if not last:
                vec.wait_ge(S["dc" + n], MATE_INC)
                g.scalar.wait_ge(S["ds" + n], MATE_INC)
                windows(t + 1, dq[:, 0:144], dp[:, 0:144], T.cl, (S["ds" + n], MATE_INC))
            else:
                g.tensor.wait_ge(S["dc" + n], MATE_INC)
                g.tensor.wait_ge(S["ds" + n], MATE_INC)
            store(t, (S["dc" + n], MATE_INC), (S["ds" + n], MATE_INC))
            if last:
                v = products(R)
                g.sync.wait_ge(S.rs, MATE_INC)
                store_nb(T.resl)
                g.scalar.wait_ge(S.s, cnt["s"])
                ystore(g.scalar, 48, 64)
                g.sync.wait_ge(S.v, v)
                ystore(g.sync, 112, 128)
    g.sync.wait_ge(S.st, cnt["st"])
    g.scalar.wait_ge(S.sty, cnt["sty"])
    g.wait_ge(S.ls, cnt["ls"])
    g.wait_ge(S.v, cnt["v"])
    g.wait_ge(S.s, cnt["s"])
